import numpy as np
import ml_dtypes


def mxq(x, axis, fmt="e4m3"):
    dtype, down = {"e4m3": (ml_dtypes.float8_e4m3fn, 7), "e5m2": (ml_dtypes.float8_e5m2, 14)}[fmt]
    v = np.moveaxis(np.asarray(x, np.float32).astype(ml_dtypes.bfloat16).astype(np.float64), axis, -1)
    blocks = v.reshape(v.shape[:-1] + (-1, 32))
    amax = np.abs(blocks).max(-1, keepdims=True)
    byte = np.maximum(np.where(amax > 0, np.frexp(amax)[1] - 1 + 127, 0) - down, 1)
    scale = np.exp2(byte - 127.0)
    codes = (blocks / scale).astype(np.float32).astype(dtype).astype(np.float64)
    return np.moveaxis((codes * scale).reshape(v.shape), -1, axis)


WIDE = False


def mx_kscale(k):
    if not WIDE:
        return np.ones(k)
    levels = np.array([10, -10, 5, -5, 0])
    if k % 512:
        return np.exp2(np.random.permutation(np.resize(levels, k // 32))).repeat(32)
    a = np.empty((k // 512, 16))
    for p in range(k // 512):
        a[p, :8] = np.random.permutation(np.resize(levels, 8))
        for g in range(8):
            far = levels[np.abs(levels - a[p, g]) >= 10]
            a[p, g + 8] = far[np.random.randint(len(far))]
    return np.exp2(a.ravel()).repeat(32)


def f64(x):
    return np.asarray(x).astype(np.float64)


def striped(idx):
    return np.tile(np.asarray(idx).reshape(-1, 16).T, (8, 1)).astype(np.uint16)


def unstriped(offs):
    return offs[:16].T.reshape(-1).astype(np.int64)


E2M1 = np.array([0.0, 0.5, 1.0, 1.5, 2.0, 3.0, 4.0, 6.0, -0.0, -0.5, -1.0, -1.5, -2.0, -3.0, -4.0, -6.0])


def pack_weight(w, fmt):
    k, n = w.shape
    w = f64(np.asarray(w, np.float32).astype(ml_dtypes.bfloat16)).reshape(k // 32, 32, n)
    amax = np.abs(w).max(1)
    if fmt == "e4m3":
        byte = np.frexp(amax)[1] - 1 + 127 - 7
    else:
        mant, ex = np.frexp(amax / 6.0)
        byte = np.where(mant > 0.5, ex, ex - 1) + 127
    byte = np.clip(np.where(amax > 0, byte, 1), 1, 254)
    scaled = (w * np.exp2(127.0 - byte)[:, None, :]).reshape(k, n).astype(np.float32)
    by_word = np.ascontiguousarray(scaled.reshape(k // 512, 128, 4, n).transpose(0, 1, 3, 2))
    if fmt == "e4m3":
        words = by_word.astype(ml_dtypes.float8_e4m3fn).view(np.uint8)
    else:
        c = by_word.astype(ml_dtypes.float4_e2m1fn).view(np.uint8) & 0xF
        words = (c[..., 0::2] | (c[..., 1::2] << 4)).reshape(k // 512, 128, 2 * n)
    return np.ascontiguousarray(words), np.ascontiguousarray(byte.astype(np.uint8).reshape(k // 512, 16, n))


def unpack_weight(words, scales, fmt):
    g, _, n = scales.shape
    words = np.ascontiguousarray(words).reshape(g, 128, n, -1)
    if fmt == "e4m3":
        vals = words.view(ml_dtypes.float8_e4m3fn).astype(np.float64)
    else:
        nib = np.empty((g, 128, n, 4), np.uint8)
        nib[..., 0::2] = words & 0xF
        nib[..., 1::2] = words >> 4
        vals = E2M1[nib]
    vals = vals * np.repeat(np.exp2(scales.astype(np.float64) - 127.0), 8, axis=1)[..., None]
    return vals.transpose(0, 1, 3, 2).reshape(g * 512, n)


B, N, T, D, NQ = 1, 512, 2048, 1024, 512
DV = 512


def sgn(shape):
    return np.random.uniform(0.5, 2.0, shape) * np.where(np.random.standard_normal(shape) < 0, -1.0, 1.0)


def setup_inputs():
    n = np.random.standard_normal
    idx = np.random.permutation(T)[:B * N]
    s = mx_kscale(D)[:, None]
    u = mx_kscale(N)
    ut = np.ones(T)
    ut[idx] = u
    kp = pack_weight(n((D, T)) / s, "e2m1")
    return {
        "qT": (n((B, D, NQ)) * s * (1.00 / np.sqrt(D))).astype(np.float32),
        "k_words": np.ascontiguousarray(kp[0].reshape(1, 2, 128, T, 2).transpose(0, 2, 3, 1, 4)).reshape(1, 128, T, 4),
        "k_scales": kp[1],
        "vT": (n((DV, T)) / ut).astype(np.float32),
        "us": (sgn((B, N, 1)) * u[:, None]).astype(np.float32),
        "rs": (n((B, NQ, DV))).astype(np.float32),
        "offs": striped(idx),
    }


def reference(qT, k_words, k_scales, vT, us, rs, offs):
    idx = unstriped(offs)
    pick = lambda x, which: x[:, which].reshape(x.shape[0], B, -1).transpose(1, 0, 2)
    k = unpack_weight(k_words.reshape(1, 128, T, 2, 2).transpose(0, 3, 1, 2, 4).reshape(2, 128, 2 * T), k_scales, "e2m1")
    kg = pick(k, idx)
    qq = mxq(f64(qT), 1, "e4m3")
    a = kg.transpose(0, 2, 1) @ qq
    y = np.square(np.maximum(a, 0.0)) * f64(us)
    wq = mxq(y, 1, "e4m3")
    o = wq.transpose(0, 2, 1) @ mxq(pick(f64(vT), idx).transpose(0, 2, 1), 1, "e4m3")
    r_ = o + f64(rs)
    return r_

@@ -1,0 +1,202 @@
+from contextlib import ExitStack
+
+import concourse.mybir as mybir
+from concourse.masks import make_identity
+
+F32 = mybir.dt.float32
+BF16 = mybir.dt.bfloat16
+I32 = mybir.dt.int32
+U32 = mybir.dt.uint32
+U16 = mybir.dt.uint16
+U8 = mybir.dt.uint8
+FP8X4 = mybir.dt.float8_e4m3fn_x4
+FP4X4 = mybir.dt.float4_e2m1fn_x4
+ACT = mybir.ActivationFunctionType
+ALU = mybir.AluOpType
+
+P = 128
+PACK = 4
+SLOTS, NEURONS, D, NQ, DV = 512, 2048, 1024, 512, 512
+PASSES = D // (P * PACK)
+Q_TILES = NQ // P
+E_BLOCKS = DV // P
+EARLY = DV - P
+
+FLOPS = 2 * SLOTS * NQ * (D + DV)
+
+
+def tile_attend_mlp_relu2_topk_kernel(tc, qT, k_words, k_scales, vT, us, rs, offs, out):
+    nc = tc.nc
+    with ExitStack() as ctx:
+        keep = ctx.enter_context(tc.tile_pool(name="keep", bufs=1))
+        psum = ctx.enter_context(tc.psum_pool(name="psum", bufs=1))
+
+        def sbuf(shape, dtype, name):
+            return keep.tile(shape, dtype, name=name, align_bytes=64)
+
+        offsets = keep.tile([P, SLOTS // 16], U16, name="offsets")
+        nc.sync.dma_start(offsets[:], offs)
+        kw_pool = sbuf([P, NEURONS], I32, "kw_pool")
+        nc.sync.dma_start(out=kw_pool[:], in_=k_words[0].rearrange("p n b -> p (n b)").bitcast(I32))
+        ks_pool = sbuf([P, PASSES, NEURONS], U8, "ks_pool")
+        nc.vector.memset(ks_pool[:].rearrange("p o n -> p (o n)").bitcast(I32), 0)
+        for quad in range(4):
+            nc.sync.dma_start(
+                out=ks_pool[32 * quad : 32 * quad + 4, :, :].bitcast(I32),
+                in_=k_scales[:, 4 * quad : 4 * quad + 4, :].rearrange("o f n -> f o n").bitcast(I32),
+            )
+        q_raw = []
+        for o in range(PASSES):
+            tile = sbuf([P, PACK, NQ], F32, f"q_raw{o}")
+            nc.sync.dma_start(out=tile[:], in_=qT[0, 512 * o : 512 * (o + 1), :].rearrange("(p t) q -> p t q", t=PACK))
+            q_raw.append(tile)
+        us_cols = sbuf([P, PACK], F32, "us_cols")
+        nc.sync.dma_start(out=us_cols[:], in_=us[0].rearrange("(p t) one -> p (t one)", t=PACK))
+        v_pool = [sbuf([P, NEURONS], F32, f"v_pool{j}") for j in range(E_BLOCKS)]
+        rs_sb = sbuf([P, Q_TILES, DV], F32, "rs_sb")
+        for j in range(E_BLOCKS - 1):
+            nc.sync.dma_start(out=v_pool[j][:], in_=vT[P * j : P * (j + 1), :])
+        for c in range(0):
+            nc.sync.dma_start(out=rs_sb[:, c, :], in_=rs[0, P * c : P * (c + 1), :])
+        nc.sync.dma_start(out=v_pool[3][:], in_=vT[P * 3 : P * 4, :])
+        for c in range(0, Q_TILES):
+            nc.sync.dma_start(out=rs_sb[:, c, :], in_=rs[0, P * c : P * (c + 1), :])
+
+        ident = sbuf([P, P], F32, "ident")
+        make_identity(nc, ident[:])
+
+        kw_listed = sbuf([P, SLOTS], U32, "kw_listed")
+        nc.vector.tensor_copy(kw_listed[:], kw_pool[:].bitcast(U32).indirect(offsets[:]))
+        kw_dealt = sbuf([P, PASSES * SLOTS * 2], U8, "kw_dealt")
+        nc.vector.tensor_copy(
+            kw_dealt[:].bitcast(U16).rearrange("p (o t m) -> p o m t", o=PASSES, t=PACK),
+            kw_listed[:].bitcast(U16).rearrange("p (m t o) -> p o m t", o=PASSES, t=PACK),
+        )
+        ks_listed = sbuf([P, PASSES, SLOTS], U8, "ks_listed")
+        for o in range(PASSES):
+            nc.vector.tensor_copy(ks_listed[:, o, :], ks_pool[:, o, :].indirect(offsets[:]))
+        ks_dealt = sbuf([P, PASSES * SLOTS], U8, "ks_dealt")
+        nc.vector.tensor_copy(
+            ks_dealt[:].rearrange("p (o t m) -> p o m t", o=PASSES, t=PACK),
+            ks_listed[:].rearrange("p o (m t) -> p o m t", t=PACK),
+        )
+
+        q_codes = sbuf([P, PASSES, NQ], U32, "q_codes")
+        q_scales = sbuf([P, PASSES, NQ], U8, "q_scales")
+
+        def group_q(o, q0, width, copy):
+            grouped = sbuf([P, width * PACK], BF16, f"q_grouped{o}_{q0}")
+            copy(
+                out=grouped[:].rearrange("p (c i t) -> p c t i", i=4, t=PACK),
+                in_=q_raw[o][:, :, q0 : q0 + width].rearrange("p t (c i) -> p c t i", i=4),
+            )
+            nc.vector.quantize_mx(
+                out=q_codes[:, o, q0 : q0 + width].bitcast(FP8X4),
+                scales=q_scales[:, o, q0 : q0 + width],
+                in_=grouped[:],
+            )
+
+        group_q(0, 0, NQ, nc.scalar.copy)
+        for c in range(Q_TILES):
+            group_q(1, P * c, P, nc.scalar.copy if c < 4 else nc.vector.tensor_copy)
+
+        y_grouped = [sbuf([P, 2, P, PACK], BF16, f"y_grouped{h}") for h in range(2)]
+        for c in range(Q_TILES):
+            cols = slice(P * c, P * (c + 1))
+            a_bank = psum.tile([P, PACK, P], F32, name=f"bank{c}")
+            for t in range(PACK):
+                for o in range(PASSES):
+                    at = (o * PACK + t) * P
+                    nc.tensor.matmul_mx(
+                        out=a_bank[:, t, :],
+                        lhsT=kw_dealt[:, 2 * at : 2 * (at + P)].bitcast(FP4X4),
+                        lhsT_scale=ks_dealt[:, at : at + P],
+                        rhs=q_codes[:, o, cols].bitcast(FP8X4),
+                        rhs_scale=q_scales[:, o, cols],
+                        start=(o == 0),
+                        stop=(o == PASSES - 1),
+                    )
+            relu = sbuf([P, P, PACK], F32, f"relu{c}")
+            nc.scalar.activation(out=relu[:], in_=a_bank[:].rearrange("p t q -> p q t"), func=ACT.Relu)
+            squared = sbuf([P, P, PACK], F32, f"squared{c}")
+            nc.scalar.activation(out=squared[:], in_=relu[:], func=ACT.Square)
+            (nc.gpsimd if c < 4 else nc.vector).tensor_tensor(
+                out=y_grouped[c // 2][:, c % 2, :, :],
+                in0=squared[:],
+                in1=us_cols[:].unsqueeze(1).to_broadcast([P, P, PACK]),
+                op=ALU.mult,
+            )
+
+        listed = []
+        for j in range(E_BLOCKS):
+            tile = sbuf([P, SLOTS], BF16, f"v_listed{j}")
+            nc.vector.tensor_copy(tile[:], v_pool[j][:].indirect(offsets[:]))
+            listed.append(tile)
+
+        code_slots = {}
+        shared = sbuf([P, 256], U32, "v_pool2")
+        code_slots["y01"] = shared[:, 0:256]
+        shared = sbuf([P, 640], U32, "v_pool3")
+        code_slots["v01"] = shared[:, 0:256]
+        code_slots["v2"] = shared[:, 256:384]
+        code_slots["y23"] = shared[:, 384:640]
+        shared = sbuf([P, 128], U32, "v_codes3")
+        code_slots["v_codes3"] = shared[:, 0:128]
+
+        def quantize(grouped, width, codes_name, scales_name):
+            codes = code_slots[codes_name]
+            scales = sbuf([P, width], U8, scales_name)
+            nc.vector.quantize_mx(out=codes.bitcast(FP8X4), scales=scales[:], in_=grouped)
+            return codes, scales
+
+        def quantize_v(blocks, bank, codes_name):
+            turned = psum.tile([P, len(blocks), 2, P], F32, name=bank)
+            for n, j in enumerate(blocks):
+                words = listed[j][:].bitcast(F32)
+                for u in range(2):
+                    nc.tensor.transpose(turned[:, n, u, :], words[:, u : 2 * P : 2], ident[:])
+            grouped = sbuf([P, len(blocks) * P * PACK], BF16, f"v_grouped{blocks[0]}")
+            nc.scalar.copy(
+                out=grouped[:].bitcast(F32).rearrange("p (n e u) -> p n e u", u=2, e=P),
+                in_=turned[:].rearrange("p n u e -> p n e u"),
+            )
+            return quantize(grouped[:], len(blocks) * P, codes_name, f"v_scales{blocks[0]}")
+
+        def second_product(acc, c, v_mx):
+            y_codes, y_scales = y_mx[c // 2]
+            cols = slice(P * (c % 2), P * (c % 2 + 1))
+            nc.tensor.matmul_mx(
+                out=acc,
+                lhsT=y_codes[:, cols].bitcast(FP8X4),
+                lhsT_scale=y_scales[:, cols],
+                rhs=v_mx[0].bitcast(FP8X4),
+                rhs_scale=v_mx[1][:],
+                start=True,
+                stop=True,
+            )
+
+        y_mx = [quantize(y_grouped[0][:].rearrange("p c q t -> p (c q t)"), 2 * P, "y01", "y_scales0")]
+        v01 = quantize_v([0, 1], "bank3", "v01")
+        v2 = quantize_v([2], "bank2", "v2")
+        y_mx.append(quantize(y_grouped[1][:].rearrange("p c q t -> p (c q t)"), 2 * P, "y23", "y_scales1"))
+        v3 = quantize_v([3], "bank4", "v_codes3")
+        o_banks = []
+        for c in range(Q_TILES):
+            o_bank = psum.tile([P, DV], F32, name=f"bank{(0, 1, 6, 7)[c]}")
+            second_product(o_bank[:, 0 : 2 * P], c, v01)
+            second_product(o_bank[:, 2 * P : EARLY], c, v2)
+            o_banks.append(o_bank)
+
+        def finish_early(c):
+            result = sbuf([P, EARLY], F32, f"result{c}")
+            nc.vector.tensor_tensor(out=result[:], in0=o_banks[c][:, 0:EARLY], in1=rs_sb[:, c, 0:EARLY], op=ALU.add)
+            nc.sync.dma_start(out=out[0, P * c : P * (c + 1), 0:EARLY], in_=result[:])
+
+        for c in range(Q_TILES):
+            finish_early(c)
+        last_bank = psum.tile([P, Q_TILES, P], F32, name="bank5")
+        for c in range(Q_TILES):
+            second_product(last_bank[:, c, :], c, v3)
+        last = sbuf([P, Q_TILES, P], F32, "last")
+        nc.vector.tensor_tensor(out=last[:], in0=last_bank[:], in1=rs_sb[:, :, EARLY:DV], op=ALU.add)
+        nc.sync.dma_start(out=out[0].rearrange("(c p) e -> p c e", p=P)[:, :, EARLY:DV], in_=last[:])

@@ -38,13 +38,16 @@ def tile_attend_mlp_relu2_topk_kernel(tc, qT, k_words, k_scales, vT, us, rs, off
         nc.sync.dma_start(offsets[:], offs)
         kw_pool = sbuf([P, NEURONS], I32, "kw_pool")
         nc.sync.dma_start(out=kw_pool[:], in_=k_words[0].rearrange("p n b -> p (n b)").bitcast(I32))
-        ks_pool = sbuf([P, PASSES, NEURONS], U8, "ks_pool")
-        nc.vector.memset(ks_pool[:].rearrange("p o n -> p (o n)").bitcast(I32), 0)
+        ks_pool = sbuf([P, NEURONS], U8, "ks_pool")
+        nc.vector.memset(ks_pool[:].bitcast(I32), 0)
+        ks_moved = sbuf([P, SLOTS], U8, "ks_moved")
+        nc.vector.memset(ks_moved[:].bitcast(I32), 0)
         for quad in range(4):
             nc.sync.dma_start(
-                out=ks_pool[32 * quad : 32 * quad + 4, :, :].bitcast(I32),
-                in_=k_scales[:, 4 * quad : 4 * quad + 4, :].rearrange("o f n -> f o n").bitcast(I32),
+                out=ks_pool[32 * quad : 32 * quad + 4, :].bitcast(I32),
+                in_=k_scales[0, 4 * quad : 4 * quad + 4, :].bitcast(I32),
             )
+        nc.sync.dma_start(out=ks_pool[4:P:8, :].bitcast(I32), in_=k_scales[1].bitcast(I32))
         q_raw = []
         for o in range(PASSES):
             tile = sbuf([P, PACK, NQ], F32, f"q_raw{o}")
@@ -52,34 +55,29 @@ def tile_attend_mlp_relu2_topk_kernel(tc, qT, k_words, k_scales, vT, us, rs, off
             q_raw.append(tile)
         us_cols = sbuf([P, PACK], F32, "us_cols")
         nc.sync.dma_start(out=us_cols[:], in_=us[0].rearrange("(p t) one -> p (t one)", t=PACK))
-        v_pool = [sbuf([P, NEURONS], F32, f"v_pool{j}") for j in range(E_BLOCKS)]
-        rs_sb = sbuf([P, Q_TILES, DV], F32, "rs_sb")
-        for j in range(E_BLOCKS - 1):
-            nc.sync.dma_start(out=v_pool[j][:], in_=vT[P * j : P * (j + 1), :])
-        for c in range(0):
-            nc.sync.dma_start(out=rs_sb[:, c, :], in_=rs[0, P * c : P * (c + 1), :])
-        nc.sync.dma_start(out=v_pool[3][:], in_=vT[P * 3 : P * 4, :])
-        for c in range(0, Q_TILES):
-            nc.sync.dma_start(out=rs_sb[:, c, :], in_=rs[0, P * c : P * (c + 1), :])
-
-        ident = sbuf([P, P], F32, "ident")
-        make_identity(nc, ident[:])
-
-        kw_listed = sbuf([P, SLOTS], U32, "kw_listed")
+        ks_listed = sbuf([P, SLOTS], U8, "ks_listed")
+        nc.vector.tensor_copy(ks_listed[:], ks_pool[:].indirect(offsets[:]))
+        ks_dealt = sbuf([P, SLOTS], U8, "ks_dealt")
+        nc.vector.tensor_copy(
+            ks_dealt[:].rearrange("p (t m) -> p t m", t=PACK),
+            ks_listed[:].rearrange("p (m t) -> p t m", t=PACK),
+        )
+        for quad in range(4):
+            nc.sync.dma_start(
+                out=ks_moved[32 * quad : 32 * quad + 4, :].bitcast(I32),
+                in_=ks_dealt[32 * quad + 4 : 32 * (quad + 1) : 8, :].bitcast(I32),
+            )
+        ks_planes = [ks_dealt, ks_moved]
+        kw_listed = sbuf([P, SLOTS], U32, "ks_pool")
         nc.vector.tensor_copy(kw_listed[:], kw_pool[:].bitcast(U32).indirect(offsets[:]))
         kw_dealt = sbuf([P, PASSES * SLOTS * 2], U8, "kw_dealt")
         nc.vector.tensor_copy(
             kw_dealt[:].bitcast(U16).rearrange("p (o t m) -> p o m t", o=PASSES, t=PACK),
             kw_listed[:].bitcast(U16).rearrange("p (m t o) -> p o m t", o=PASSES, t=PACK),
         )
-        ks_listed = sbuf([P, PASSES, SLOTS], U8, "ks_listed")
-        for o in range(PASSES):
-            nc.vector.tensor_copy(ks_listed[:, o, :], ks_pool[:, o, :].indirect(offsets[:]))
-        ks_dealt = sbuf([P, PASSES * SLOTS], U8, "ks_dealt")
-        nc.vector.tensor_copy(
-            ks_dealt[:].rearrange("p (o t m) -> p o m t", o=PASSES, t=PACK),
-            ks_listed[:].rearrange("p o (m t) -> p o m t", t=PACK),
-        )
+
+        ident = sbuf([P, P], F32, "ident")
+        make_identity(nc, ident[:])
 
         q_codes = sbuf([P, PASSES, NQ], U32, "q_codes")
         q_scales = sbuf([P, PASSES, NQ], U8, "q_scales")
@@ -100,7 +98,19 @@ def tile_attend_mlp_relu2_topk_kernel(tc, qT, k_words, k_scales, vT, us, rs, off
         for c in range(Q_TILES):
             group_q(1, P * c, P, nc.scalar.copy if c < 4 else nc.vector.tensor_copy)
 
-        y_grouped = [sbuf([P, 2, P, PACK], BF16, f"y_grouped{h}") for h in range(2)]
+        v_pool = [sbuf([P, NEURONS], F32, name) for name in ("ks_listed", "kw_pool", "q_raw0", "q_raw1")]
+        for j in range(E_BLOCKS):
+            nc.sync.dma_start(out=v_pool[j][:], in_=vT[P * j : P * (j + 1), :])
+        listed = []
+        for j in range(E_BLOCKS):
+            tile = sbuf([P, SLOTS], BF16, f"v_listed{j}")
+            nc.vector.tensor_copy(tile[:], v_pool[j][:].indirect(offsets[:]))
+            listed.append(tile)
+        rs_sb = sbuf([P, Q_TILES, DV], F32, "ks_listed")
+        for c in range(Q_TILES):
+            nc.sync.dma_start(out=rs_sb[:, c, :], in_=rs[0, P * c : P * (c + 1), :])
+
+        y_grouped = [sbuf([P, 2, P, PACK], BF16, name) for name in ("y_grouped0", "y_grouped1")]
         for c in range(Q_TILES):
             cols = slice(P * c, P * (c + 1))
             a_bank = psum.tile([P, PACK, P], F32, name=f"bank{c}")
@@ -110,13 +120,13 @@ def tile_attend_mlp_relu2_topk_kernel(tc, qT, k_words, k_scales, vT, us, rs, off
                     nc.tensor.matmul_mx(
                         out=a_bank[:, t, :],
                         lhsT=kw_dealt[:, 2 * at : 2 * (at + P)].bitcast(FP4X4),
-                        lhsT_scale=ks_dealt[:, at : at + P],
+                        lhsT_scale=ks_planes[o][:, P * t : P * (t + 1)],
                         rhs=q_codes[:, o, cols].bitcast(FP8X4),
                         rhs_scale=q_scales[:, o, cols],
                         start=(o == 0),
                         stop=(o == PASSES - 1),
                     )
-            relu = sbuf([P, P, PACK], F32, f"relu{c}")
+            relu = sbuf([P, P, PACK], F32, "relu")
             nc.scalar.activation(out=relu[:], in_=a_bank[:].rearrange("p t q -> p q t"), func=ACT.Relu)
             squared = sbuf([P, P, PACK], F32, f"squared{c}")
             nc.scalar.activation(out=squared[:], in_=relu[:], func=ACT.Square)
@@ -127,16 +137,10 @@ def tile_attend_mlp_relu2_topk_kernel(tc, qT, k_words, k_scales, vT, us, rs, off
                 op=ALU.mult,
             )
 
-        listed = []
-        for j in range(E_BLOCKS):
-            tile = sbuf([P, SLOTS], BF16, f"v_listed{j}")
-            nc.vector.tensor_copy(tile[:], v_pool[j][:].indirect(offsets[:]))
-            listed.append(tile)
-
         code_slots = {}
-        shared = sbuf([P, 256], U32, "v_pool2")
+        shared = sbuf([P, 256], U32, "q_raw0")
         code_slots["y01"] = shared[:, 0:256]
-        shared = sbuf([P, 640], U32, "v_pool3")
+        shared = sbuf([P, 640], U32, "q_raw1")
         code_slots["v01"] = shared[:, 0:256]
         code_slots["v2"] = shared[:, 256:384]
         code_slots["y23"] = shared[:, 384:640]
@@ -149,7 +153,7 @@ def tile_attend_mlp_relu2_topk_kernel(tc, qT, k_words, k_scales, vT, us, rs, off
             nc.vector.quantize_mx(out=codes.bitcast(FP8X4), scales=scales[:], in_=grouped)
             return codes, scales
 
-        def quantize_v(blocks, bank, codes_name):
+        def turn_v(blocks, bank):
             turned = psum.tile([P, len(blocks), 2, P], F32, name=bank)
             for n, j in enumerate(blocks):
                 words = listed[j][:].bitcast(F32)
@@ -160,7 +164,7 @@ def tile_attend_mlp_relu2_topk_kernel(tc, qT, k_words, k_scales, vT, us, rs, off
                 out=grouped[:].bitcast(F32).rearrange("p (n e u) -> p n e u", u=2, e=P),
                 in_=turned[:].rearrange("p n u e -> p n e u"),
             )
-            return quantize(grouped[:], len(blocks) * P, codes_name, f"v_scales{blocks[0]}")
+            return grouped
 
         def second_product(acc, c, v_mx):
             y_codes, y_scales = y_mx[c // 2]
@@ -176,10 +180,10 @@ def tile_attend_mlp_relu2_topk_kernel(tc, qT, k_words, k_scales, vT, us, rs, off
             )
 
         y_mx = [quantize(y_grouped[0][:].rearrange("p c q t -> p (c q t)"), 2 * P, "y01", "y_scales0")]
-        v01 = quantize_v([0, 1], "bank3", "v01")
-        v2 = quantize_v([2], "bank2", "v2")
+        v01 = quantize(turn_v([0, 1], "bank3")[:], 2 * P, "v01", "v_scales0")
+        v2 = quantize(turn_v([2], "bank2")[:], P, "v2", "v_scales2")
         y_mx.append(quantize(y_grouped[1][:].rearrange("p c q t -> p (c q t)"), 2 * P, "y23", "y_scales1"))
-        v3 = quantize_v([3], "bank4", "v_codes3")
+        v3_grouped = turn_v([3], "bank4")
         o_banks = []
         for c in range(Q_TILES):
             o_bank = psum.tile([P, DV], F32, name=f"bank{(0, 1, 6, 7)[c]}")
@@ -192,11 +196,14 @@ def tile_attend_mlp_relu2_topk_kernel(tc, qT, k_words, k_scales, vT, us, rs, off
             nc.vector.tensor_tensor(out=result[:], in0=o_banks[c][:, 0:EARLY], in1=rs_sb[:, c, 0:EARLY], op=ALU.add)
             nc.sync.dma_start(out=out[0, P * c : P * (c + 1), 0:EARLY], in_=result[:])
 
-        for c in range(Q_TILES):
-            finish_early(c)
+        finish_early(0)
+        finish_early(1)
+        v3 = quantize(v3_grouped[:], P, "v_codes3", "v_scales3")
+        finish_early(2)
         last_bank = psum.tile([P, Q_TILES, P], F32, name="bank5")
         for c in range(Q_TILES):
             second_product(last_bank[:, c, :], c, v3)
         last = sbuf([P, Q_TILES, P], F32, "last")
         nc.vector.tensor_tensor(out=last[:], in0=last_bank[:], in1=rs_sb[:, :, EARLY:DV], op=ALU.add)
         nc.sync.dma_start(out=out[0].rearrange("(c p) e -> p c e", p=P)[:, :, EARLY:DV], in_=last[:])
+        finish_early(3)

@@ -20,7 +20,7 @@ SLOTS, NEURONS, D, NQ, DV = 512, 2048, 1024, 512, 512
 PASSES = D // (P * PACK)
 Q_TILES = NQ // P
 E_BLOCKS = DV // P
-EARLY = DV - P
+HALF = DV // 2
 
 FLOPS = 2 * SLOTS * NQ * (D + DV)
 
@@ -36,25 +36,19 @@ def tile_attend_mlp_relu2_topk_kernel(tc, qT, k_words, k_scales, vT, us, rs, off
 
         offsets = keep.tile([P, SLOTS // 16], U16, name="offsets")
         nc.sync.dma_start(offsets[:], offs)
+        ks_pool = sbuf([P, NEURONS], U8, "ks_pool")
+        nc.vector.memset(ks_pool[0:96, :].bitcast(I32), 0)
+        nc.sync.dma_start(out=ks_pool[96:P, :].bitcast(I32), in_=k_scales.bitcast(I32).rearrange("o f n -> f o n"))
         kw_pool = sbuf([P, NEURONS], I32, "kw_pool")
         nc.sync.dma_start(out=kw_pool[:], in_=k_words[0].rearrange("p n b -> p (n b)").bitcast(I32))
-        ks_pool = sbuf([P, NEURONS], U8, "ks_pool")
-        nc.vector.memset(ks_pool[:].bitcast(I32), 0)
-        ks_moved = sbuf([P, SLOTS], U8, "ks_moved")
-        nc.vector.memset(ks_moved[:].bitcast(I32), 0)
-        for quad in range(4):
-            nc.sync.dma_start(
-                out=ks_pool[32 * quad : 32 * quad + 4, :].bitcast(I32),
-                in_=k_scales[0, 4 * quad : 4 * quad + 4, :].bitcast(I32),
-            )
-        nc.sync.dma_start(out=ks_pool[4:P:8, :].bitcast(I32), in_=k_scales[1].bitcast(I32))
-        q_raw = []
-        for o in range(PASSES):
-            tile = sbuf([P, PACK, NQ], F32, f"q_raw{o}")
-            nc.sync.dma_start(out=tile[:], in_=qT[0, 512 * o : 512 * (o + 1), :].rearrange("(p t) q -> p t q", t=PACK))
-            q_raw.append(tile)
+        ks_planes = sbuf([P, PASSES * SLOTS], U8, "ks_planes")
+        nc.vector.memset(ks_planes[:].bitcast(I32), 0)
+        q_rows = qT[0].rearrange("(o p t) q -> o p t q", o=PASSES, t=PACK)
+        q_raw0 = sbuf([P, PACK, NQ], F32, "q_raw0")
+        nc.sync.dma_start(out=q_raw0[:], in_=q_rows[0])
         us_cols = sbuf([P, PACK], F32, "us_cols")
         nc.sync.dma_start(out=us_cols[:], in_=us[0].rearrange("(p t) one -> p (t one)", t=PACK))
+
         ks_listed = sbuf([P, SLOTS], U8, "ks_listed")
         nc.vector.tensor_copy(ks_listed[:], ks_pool[:].indirect(offsets[:]))
         ks_dealt = sbuf([P, SLOTS], U8, "ks_dealt")
@@ -64,10 +58,12 @@ def tile_attend_mlp_relu2_topk_kernel(tc, qT, k_words, k_scales, vT, us, rs, off
         )
         for quad in range(4):
             nc.sync.dma_start(
-                out=ks_moved[32 * quad : 32 * quad + 4, :].bitcast(I32),
-                in_=ks_dealt[32 * quad + 4 : 32 * (quad + 1) : 8, :].bitcast(I32),
+                out=ks_planes[32 * quad : 32 * quad + 4, :].bitcast(I32).rearrange("p (o n) -> p o n", o=PASSES),
+                in_=ks_dealt[96 + 8 * quad : 96 + 8 * (quad + 1), :].bitcast(I32),
             )
-        ks_planes = [ks_dealt, ks_moved]
+        q_raw1 = sbuf([P, 2, PACK, 2 * P], F32, "ks_listed")
+        for h in range(2):
+            nc.sync.dma_start(out=q_raw1[:, h, :, :], in_=q_rows[1, :, :, 2 * P * h : 2 * P * (h + 1)])
         kw_listed = sbuf([P, SLOTS], U32, "ks_pool")
         nc.vector.tensor_copy(kw_listed[:], kw_pool[:].bitcast(U32).indirect(offsets[:]))
         kw_dealt = sbuf([P, PASSES * SLOTS * 2], U8, "kw_dealt")
@@ -79,131 +75,181 @@ def tile_attend_mlp_relu2_topk_kernel(tc, qT, k_words, k_scales, vT, us, rs, off
         ident = sbuf([P, P], F32, "ident")
         make_identity(nc, ident[:])
 
-        q_codes = sbuf([P, PASSES, NQ], U32, "q_codes")
-        q_scales = sbuf([P, PASSES, NQ], U8, "q_scales")
+        q_mx = {}
 
-        def group_q(o, q0, width, copy):
-            grouped = sbuf([P, width * PACK], BF16, f"q_grouped{o}_{q0}")
+        def round_q(raw, copy, name):
+            grouped = sbuf([P, raw.shape[2] * PACK], BF16, name)
             copy(
                 out=grouped[:].rearrange("p (c i t) -> p c t i", i=4, t=PACK),
-                in_=q_raw[o][:, :, q0 : q0 + width].rearrange("p t (c i) -> p c t i", i=4),
+                in_=raw.rearrange("p t (c i) -> p c t i", i=4),
             )
-            nc.vector.quantize_mx(
-                out=q_codes[:, o, q0 : q0 + width].bitcast(FP8X4),
-                scales=q_scales[:, o, q0 : q0 + width],
-                in_=grouped[:],
-            )
+            return grouped
 
-        group_q(0, 0, NQ, nc.scalar.copy)
-        for c in range(Q_TILES):
-            group_q(1, P * c, P, nc.scalar.copy if c < 4 else nc.vector.tensor_copy)
+        def quantize(grouped, width, name, codes=None):
+            if codes is None:
+                codes = sbuf([P, width], U32, f"{name}_codes")
+            scales = sbuf([P, width], U8, f"{name}_scales")
+            nc.vector.quantize_mx(out=codes[:].bitcast(FP8X4), scales=scales[:], in_=grouped)
+            return codes, scales
 
-        v_pool = [sbuf([P, NEURONS], F32, name) for name in ("ks_listed", "kw_pool", "q_raw0", "q_raw1")]
-        for j in range(E_BLOCKS):
-            nc.sync.dma_start(out=v_pool[j][:], in_=vT[P * j : P * (j + 1), :])
-        listed = []
-        for j in range(E_BLOCKS):
-            tile = sbuf([P, SLOTS], BF16, f"v_listed{j}")
-            nc.vector.tensor_copy(tile[:], v_pool[j][:].indirect(offsets[:]))
-            listed.append(tile)
-        rs_sb = sbuf([P, Q_TILES, DV], F32, "ks_listed")
-        for c in range(Q_TILES):
-            nc.sync.dma_start(out=rs_sb[:, c, :], in_=rs[0, P * c : P * (c + 1), :])
+        def quantize_q0(h, grouped, codes=None):
+            codes, scales = quantize(grouped[:], 2 * P, f"q0_{h}", codes)
+            for n in range(2):
+                q_mx[(0, 2 * h + n)] = (codes[:, P * n : P * (n + 1)], scales[:, P * n : P * (n + 1)])
 
-        y_grouped = [sbuf([P, 2, P, PACK], BF16, name) for name in ("y_grouped0", "y_grouped1")]
+        def round_q1(c, copy):
+            return round_q(q_raw1[:, c // 2, :, P * (c % 2) : P * (c % 2 + 1)], copy, f"q_grouped1_{c}")
+
+        def quantize_q1(c, grouped):
+            codes, scales = quantize(grouped[:], P, f"q1_{c}")
+            q_mx[(1, c)] = (codes[:], scales[:])
+
+        q0_low = round_q(q_raw0[:, :, 0 : 2 * P], nc.vector.tensor_copy, "q_grouped0_0")
+        q0_high = round_q(q_raw0[:, :, 2 * P : NQ], nc.scalar.copy, "q_grouped0_1")
+        quantize_q0(0, q0_low)
+        q1 = [round_q1(0, nc.vector.tensor_copy), round_q1(1, nc.scalar.copy)]
+        quantize_q1(0, q1[0])
+        quantize_q1(1, q1[1])
+        quantize_q0(1, q0_high, sbuf([P, 2 * P], U32, "q_grouped1_1"))
+        q1.extend([round_q1(2, nc.vector.tensor_copy), round_q1(3, nc.vector.tensor_copy)])
+        quantize_q1(2, q1[2])
+        quantize_q1(3, q1[3])
+
+        a_banks = [psum.tile([P, PACK, P], F32, name=f"bank{c}") for c in range(Q_TILES)]
         for c in range(Q_TILES):
-            cols = slice(P * c, P * (c + 1))
-            a_bank = psum.tile([P, PACK, P], F32, name=f"bank{c}")
-            for t in range(PACK):
-                for o in range(PASSES):
+            for o in range(PASSES):
+                for t in range(PACK):
                     at = (o * PACK + t) * P
                     nc.tensor.matmul_mx(
-                        out=a_bank[:, t, :],
+                        out=a_banks[c][:, t, :],
                         lhsT=kw_dealt[:, 2 * at : 2 * (at + P)].bitcast(FP4X4),
-                        lhsT_scale=ks_planes[o][:, P * t : P * (t + 1)],
-                        rhs=q_codes[:, o, cols].bitcast(FP8X4),
-                        rhs_scale=q_scales[:, o, cols],
-                        start=(o == 0),
-                        stop=(o == PASSES - 1),
+                        lhsT_scale=ks_planes[:, at : at + P],
+                        rhs=q_mx[(o, c)][0].bitcast(FP8X4),
+                        rhs_scale=q_mx[(o, c)][1],
+                        start=(o == 0 and t == 0),
+                        stop=(o == PASSES - 1 and t == PACK - 1),
                     )
+
+        v_pool = [sbuf([P, NEURONS], F32, name) for name in ("kw_pool", "ks_pool", "q_raw0", "ks_listed")]
+        for j in range(E_BLOCKS):
+            nc.sync.dma_start(out=v_pool[j][:], in_=vT[P * j : P * (j + 1), :])
+
+        def weigh_on_gpsimd(c, grouped):
             relu = sbuf([P, P, PACK], F32, "relu")
-            nc.scalar.activation(out=relu[:], in_=a_bank[:].rearrange("p t q -> p q t"), func=ACT.Relu)
+            nc.scalar.activation(out=relu[:], in_=a_banks[c][:].rearrange("p t q -> p q t"), func=ACT.Relu)
             squared = sbuf([P, P, PACK], F32, f"squared{c}")
             nc.scalar.activation(out=squared[:], in_=relu[:], func=ACT.Square)
-            (nc.gpsimd if c < 4 else nc.vector).tensor_tensor(
-                out=y_grouped[c // 2][:, c % 2, :, :],
+            nc.gpsimd.tensor_tensor(
+                out=grouped,
                 in0=squared[:],
                 in1=us_cols[:].unsqueeze(1).to_broadcast([P, P, PACK]),
                 op=ALU.mult,
             )
 
-        code_slots = {}
-        shared = sbuf([P, 256], U32, "q_raw0")
-        code_slots["y01"] = shared[:, 0:256]
-        shared = sbuf([P, 640], U32, "q_raw1")
-        code_slots["v01"] = shared[:, 0:256]
-        code_slots["v2"] = shared[:, 256:384]
-        code_slots["y23"] = shared[:, 384:640]
-        shared = sbuf([P, 128], U32, "v_codes3")
-        code_slots["v_codes3"] = shared[:, 0:128]
+        def scale_by_us(c):
+            scaled = sbuf([P, PACK, P], F32, f"scaled{c}")
+            for t in range(PACK):
+                nc.scalar.activation(out=scaled[:, t, :], in_=a_banks[c][:, t, :], func=ACT.Copy, scale=us_cols[:, t : t + 1])
+            return scaled
 
-        def quantize(grouped, width, codes_name, scales_name):
-            codes = code_slots[codes_name]
-            scales = sbuf([P, width], U8, scales_name)
-            nc.vector.quantize_mx(out=codes.bitcast(FP8X4), scales=scales[:], in_=grouped)
-            return codes, scales
-
-        def turn_v(blocks, bank):
-            turned = psum.tile([P, len(blocks), 2, P], F32, name=bank)
-            for n, j in enumerate(blocks):
-                words = listed[j][:].bitcast(F32)
-                for u in range(2):
-                    nc.tensor.transpose(turned[:, n, u, :], words[:, u : 2 * P : 2], ident[:])
-            grouped = sbuf([P, len(blocks) * P * PACK], BF16, f"v_grouped{blocks[0]}")
-            nc.scalar.copy(
-                out=grouped[:].bitcast(F32).rearrange("p (n e u) -> p n e u", u=2, e=P),
-                in_=turned[:].rearrange("p n u e -> p n e u"),
+        def weigh_on_vector(c, scaled, name):
+            grouped = sbuf([P, P, PACK], BF16, name)
+            nc.vector.scalar_tensor_tensor(
+                out=grouped[:],
+                in0=a_banks[c][:].rearrange("p t q -> p q t"),
+                scalar=0.0,
+                in1=scaled[:].rearrange("p t q -> p q t"),
+                op0=ALU.max,
+                op1=ALU.mult,
             )
             return grouped
 
+        def gather_v(j):
+            listed = sbuf([P, SLOTS], BF16, f"v_listed{j}")
+            nc.vector.tensor_copy(listed[:], v_pool[j][:].indirect(offsets[:]))
+            return listed
+
+        def turn_v(listed, turned, grouped):
+            words = listed[:].bitcast(F32)
+            for u in range(2):
+                nc.tensor.transpose(turned[:, u, :], words[:, u : 2 * P : 2], ident[:])
+            nc.scalar.copy(
+                out=grouped.bitcast(F32).rearrange("p (e u) -> p e u", u=2),
+                in_=turned[:].rearrange("p u e -> p e u"),
+            )
+
         def second_product(acc, c, v_mx):
-            y_codes, y_scales = y_mx[c // 2]
-            cols = slice(P * (c % 2), P * (c % 2 + 1))
+            y_codes, y_scales = y_mx[c]
             nc.tensor.matmul_mx(
                 out=acc,
-                lhsT=y_codes[:, cols].bitcast(FP8X4),
-                lhsT_scale=y_scales[:, cols],
-                rhs=v_mx[0].bitcast(FP8X4),
+                lhsT=y_codes.bitcast(FP8X4),
+                lhsT_scale=y_scales,
+                rhs=v_mx[0][:].bitcast(FP8X4),
                 rhs_scale=v_mx[1][:],
                 start=True,
                 stop=True,
             )
 
-        y_mx = [quantize(y_grouped[0][:].rearrange("p c q t -> p (c q t)"), 2 * P, "y01", "y_scales0")]
-        v01 = quantize(turn_v([0, 1], "bank3")[:], 2 * P, "v01", "v_scales0")
-        v2 = quantize(turn_v([2], "bank2")[:], P, "v2", "v_scales2")
-        y_mx.append(quantize(y_grouped[1][:].rearrange("p c q t -> p (c q t)"), 2 * P, "y23", "y_scales1"))
-        v3_grouped = turn_v([3], "bank4")
-        o_banks = []
-        for c in range(Q_TILES):
-            o_bank = psum.tile([P, DV], F32, name=f"bank{(0, 1, 6, 7)[c]}")
-            second_product(o_bank[:, 0 : 2 * P], c, v01)
-            second_product(o_bank[:, 2 * P : EARLY], c, v2)
-            o_banks.append(o_bank)
+        v01_grouped = sbuf([P, 2 * P * PACK], BF16, "v_grouped01")
+        v_grouped = [v01_grouped[:, 0 : P * PACK], v01_grouped[:, P * PACK : 2 * P * PACK]]
+        for j in (2, 3):
+            v_grouped.append(sbuf([P, P * PACK], BF16, f"v_grouped{j}")[:])
 
-        def finish_early(c):
-            result = sbuf([P, EARLY], F32, f"result{c}")
-            nc.vector.tensor_tensor(out=result[:], in0=o_banks[c][:, 0:EARLY], in1=rs_sb[:, c, 0:EARLY], op=ALU.add)
-            nc.sync.dma_start(out=out[0, P * c : P * (c + 1), 0:EARLY], in_=result[:])
+        def bring_v(j):
+            turned = psum.tile([P, 2, P], F32, name=f"bank{4 + j % 2}")
+            turn_v(gather_v(j), turned, v_grouped[j])
+
+        rs_sb = sbuf([P, Q_TILES, DV], F32, "q_grouped1_3")
+        for c in range(Q_TILES):
+            nc.sync.dma_start(out=rs_sb[:, c, :], in_=rs[0, P * c : P * (c + 1), :])
+        y_rest = sbuf([P, 3, P, PACK], BF16, "y_rest")
+        weigh_on_gpsimd(0, y_rest[:, 0, :, :])
+        scaled1 = scale_by_us(1)
+        weigh_on_gpsimd(2, y_rest[:, 1, :, :])
+        bring_v(0)
+        y1 = weigh_on_vector(1, scaled1, "kw_pool")
+        weigh_on_gpsimd(3, y_rest[:, 2, :, :])
+        bring_v(1)
+        after_v1 = sbuf([P, P], U32, "ks_pool")
+        odd1 = quantize(y1[:].rearrange("p q t -> p (q t)"), P, "y1", after_v1)
+        bring_v(2)
+        after_v2 = sbuf([P, 5 * P], U32, "q_raw0")
+        even = quantize(y_rest[:, 0:2, :, :].rearrange("p c q t -> p (c q t)"), 2 * P, "y_even", after_v2[:, 0 : 2 * P])
+        v01 = quantize(v01_grouped[:], 2 * P, "v01", after_v2[:, 2 * P : 4 * P])
+        odd3 = quantize(y_rest[:, 2, :, :].rearrange("p q t -> p (q t)"), P, "y3", after_v2[:, 4 * P : 5 * P])
+        y_mx = [
+            (even[0][:, 0:P], even[1][:, 0:P]),
+            (odd1[0][:], odd1[1][:]),
+            (even[0][:, P : 2 * P], even[1][:, P : 2 * P]),
+            (odd3[0], odd3[1][:]),
+        ]
+        out_rows = out[0].rearrange("(c p) e -> p c e", p=P)
+        early_sums = []
+        for h in range(2):
+            bank = psum.tile([P, 2, HALF], F32, name=f"bank{6 + h}")
+            for n in range(2):
+                second_product(bank[:, n, :], 2 * h + n, v01)
+            sums = sbuf([P, 2, HALF], F32, f"early_sums{h}")
+            nc.scalar.copy(out=sums[:], in_=bank[:])
+            early_sums.append(sums)
+        bring_v(3)
+        v2 = quantize(v_grouped[2], P, "v2", sbuf([P, P], U32, "ks_listed"))
+        late_banks = [psum.tile([P, 2, P], F32, name=f"bank{c}") for c in range(Q_TILES)]
+        for c in range(Q_TILES):
+            second_product(late_banks[c][:, 0, :], c, v2)
+
+        def finish_early(h):
+            result = sbuf([P, 2, HALF], F32, f"early{h}")
+            nc.vector.tensor_tensor(out=result[:], in0=early_sums[h][:], in1=rs_sb[:, 2 * h : 2 * h + 2, 0:HALF], op=ALU.add)
+            nc.sync.dma_start(out=out_rows[:, 2 * h : 2 * h + 2, 0:HALF], in_=result[:])
 
         finish_early(0)
+        v3 = quantize(v_grouped[3], P, "v3", sbuf([P, P], U32, "early_sums0"))
         finish_early(1)
-        v3 = quantize(v3_grouped[:], P, "v_codes3", "v_scales3")
-        finish_early(2)
-        last_bank = psum.tile([P, Q_TILES, P], F32, name="bank5")
         for c in range(Q_TILES):
-            second_product(last_bank[:, c, :], c, v3)
-        last = sbuf([P, Q_TILES, P], F32, "last")
-        nc.vector.tensor_tensor(out=last[:], in0=last_bank[:], in1=rs_sb[:, :, EARLY:DV], op=ALU.add)
-        nc.sync.dma_start(out=out[0].rearrange("(c p) e -> p c e", p=P)[:, :, EARLY:DV], in_=last[:])
-        finish_early(3)
+            second_product(late_banks[c][:, 1, :], c, v3)
+            late = sbuf([P, HALF], F32, f"late{c}")
+            nc.vector.tensor_tensor(
+                out=late[:], in0=late_banks[c][:].rearrange("p n e -> p (n e)"), in1=rs_sb[:, c, HALF:DV], op=ALU.add
+            )
+            nc.sync.dma_start(out=out[0, P * c : P * (c + 1), HALF:DV], in_=late[:])

@@ -61,9 +61,8 @@ def tile_attend_mlp_relu2_topk_kernel(tc, qT, k_words, k_scales, vT, us, rs, off
                 out=ks_planes[32 * quad : 32 * quad + 4, :].bitcast(I32).rearrange("p (o n) -> p o n", o=PASSES),
                 in_=ks_dealt[96 + 8 * quad : 96 + 8 * (quad + 1), :].bitcast(I32),
             )
-        q_raw1 = sbuf([P, 2, PACK, 2 * P], F32, "ks_listed")
-        for h in range(2):
-            nc.sync.dma_start(out=q_raw1[:, h, :, :], in_=q_rows[1, :, :, 2 * P * h : 2 * P * (h + 1)])
+        q_raw1 = sbuf([P, PACK, NQ], F32, "ks_listed")
+        nc.sync.dma_start(out=q_raw1[:], in_=q_rows[1])
         kw_listed = sbuf([P, SLOTS], U32, "ks_pool")
         nc.vector.tensor_copy(kw_listed[:], kw_pool[:].bitcast(U32).indirect(offsets[:]))
         kw_dealt = sbuf([P, PASSES * SLOTS * 2], U8, "kw_dealt")
@@ -98,7 +97,7 @@ def tile_attend_mlp_relu2_topk_kernel(tc, qT, k_words, k_scales, vT, us, rs, off
                 q_mx[(0, 2 * h + n)] = (codes[:, P * n : P * (n + 1)], scales[:, P * n : P * (n + 1)])
 
         def round_q1(c, copy):
-            return round_q(q_raw1[:, c // 2, :, P * (c % 2) : P * (c % 2 + 1)], copy, f"q_grouped1_{c}")
+            return round_q(q_raw1[:, :, P * c : P * (c + 1)], copy, f"q_grouped1_{c}")
 
         def quantize_q1(c, grouped):
             codes, scales = quantize(grouped[:], P, f"q1_{c}")
@@ -107,13 +106,10 @@ def tile_attend_mlp_relu2_topk_kernel(tc, qT, k_words, k_scales, vT, us, rs, off
         q0_low = round_q(q_raw0[:, :, 0 : 2 * P], nc.vector.tensor_copy, "q_grouped0_0")
         q0_high = round_q(q_raw0[:, :, 2 * P : NQ], nc.scalar.copy, "q_grouped0_1")
         quantize_q0(0, q0_low)
-        q1 = [round_q1(0, nc.vector.tensor_copy), round_q1(1, nc.scalar.copy)]
-        quantize_q1(0, q1[0])
-        quantize_q1(1, q1[1])
-        quantize_q0(1, q0_high, sbuf([P, 2 * P], U32, "q_grouped1_1"))
-        q1.extend([round_q1(2, nc.vector.tensor_copy), round_q1(3, nc.vector.tensor_copy)])
-        quantize_q1(2, q1[2])
-        quantize_q1(3, q1[3])
+        quantize_q0(1, q0_high)
+        q1 = [round_q1(c, nc.scalar.copy if c % 2 else nc.vector.tensor_copy) for c in range(Q_TILES)]
+        for c in range(Q_TILES):
+            quantize_q1(c, q1[c])
 
         a_banks = [psum.tile([P, PACK, P], F32, name=f"bank{c}") for c in range(Q_TILES)]
         for c in range(Q_TILES):

@@ -130,11 +130,14 @@ def tile_attend_mlp_relu2_topk_kernel(tc, qT, k_words, k_scales, vT, us, rs, off
         for j in range(E_BLOCKS):
             nc.sync.dma_start(out=v_pool[j][:], in_=vT[P * j : P * (j + 1), :])
 
-        def weigh_on_gpsimd(c, grouped):
-            relu = sbuf([P, P, PACK], F32, "relu")
+        def square(c):
+            relu = sbuf([P, P, PACK], F32, f"relu{c % 2}")
             nc.scalar.activation(out=relu[:], in_=a_banks[c][:].rearrange("p t q -> p q t"), func=ACT.Relu)
             squared = sbuf([P, P, PACK], F32, f"squared{c}")
             nc.scalar.activation(out=squared[:], in_=relu[:], func=ACT.Square)
+            return squared
+
+        def weigh(squared, grouped):
             nc.gpsimd.tensor_tensor(
                 out=grouped,
                 in0=squared[:],
@@ -148,17 +151,15 @@ def tile_attend_mlp_relu2_topk_kernel(tc, qT, k_words, k_scales, vT, us, rs, off
                 nc.scalar.activation(out=scaled[:, t, :], in_=a_banks[c][:, t, :], func=ACT.Copy, scale=us_cols[:, t : t + 1])
             return scaled
 
-        def weigh_on_vector(c, scaled, name):
-            grouped = sbuf([P, P, PACK], BF16, name)
+        def weigh_on_vector(c, scaled, grouped):
             nc.vector.scalar_tensor_tensor(
-                out=grouped[:],
+                out=grouped,
                 in0=a_banks[c][:].rearrange("p t q -> p q t"),
                 scalar=0.0,
                 in1=scaled[:].rearrange("p t q -> p q t"),
                 op0=ALU.max,
                 op1=ALU.mult,
             )
-            return grouped
 
         def gather_v(j):
             listed = sbuf([P, SLOTS], BF16, f"v_listed{j}")
@@ -186,11 +187,6 @@ def tile_attend_mlp_relu2_topk_kernel(tc, qT, k_words, k_scales, vT, us, rs, off
                 stop=True,
             )
 
-        v01_grouped = sbuf([P, 2 * P * PACK], BF16, "v_grouped01")
-        v_grouped = [v01_grouped[:, 0 : P * PACK], v01_grouped[:, P * PACK : 2 * P * PACK]]
-        for j in (2, 3):
-            v_grouped.append(sbuf([P, P * PACK], BF16, f"v_grouped{j}")[:])
-
         def bring_v(j):
             turned = psum.tile([P, 2, P], F32, name=f"bank{4 + j % 2}")
             turn_v(gather_v(j), turned, v_grouped[j])
@@ -198,54 +194,58 @@ def tile_attend_mlp_relu2_topk_kernel(tc, qT, k_words, k_scales, vT, us, rs, off
         rs_sb = sbuf([P, Q_TILES, DV], F32, "q_grouped1_3")
         for c in range(Q_TILES):
             nc.sync.dma_start(out=rs_sb[:, c, :], in_=rs[0, P * c : P * (c + 1), :])
-        y_rest = sbuf([P, 3, P, PACK], BF16, "y_rest")
-        weigh_on_gpsimd(0, y_rest[:, 0, :, :])
-        scaled1 = scale_by_us(1)
-        weigh_on_gpsimd(2, y_rest[:, 1, :, :])
+        y_grouped = [sbuf([P, 2, P, PACK], BF16, f"y_grouped{h}") for h in range(2)]
+        weigh_on_vector(0, scale_by_us(0), y_grouped[0][:, 0, :, :])
+        for c in range(1, Q_TILES):
+            weigh(square(c), y_grouped[c // 2][:, c % 2, :, :])
+        v01_grouped = sbuf([P, 2 * P * PACK], BF16, "relu1")
+        v_grouped = [v01_grouped[:, 0 : P * PACK], v01_grouped[:, P * PACK : 2 * P * PACK]]
+        for j in (2, 3):
+            v_grouped.append(sbuf([P, P * PACK], BF16, f"v_grouped{j}")[:])
+        y_mx = []
+
+        def quantize_y(h, codes):
+            codes, scales = quantize(y_grouped[h][:].rearrange("p c q t -> p (c q t)"), 2 * P, f"y{h}", codes)
+            y_mx.extend([(codes[:, P * n : P * (n + 1)], scales[:, P * n : P * (n + 1)]) for n in range(2)])
+
         bring_v(0)
-        y1 = weigh_on_vector(1, scaled1, "kw_pool")
-        weigh_on_gpsimd(3, y_rest[:, 2, :, :])
         bring_v(1)
-        after_v1 = sbuf([P, P], U32, "ks_pool")
-        odd1 = quantize(y1[:].rearrange("p q t -> p (q t)"), P, "y1", after_v1)
+        quantize_y(0, sbuf([P, 2 * P], U32, "ks_pool"))
         bring_v(2)
-        after_v2 = sbuf([P, 5 * P], U32, "q_raw0")
-        even = quantize(y_rest[:, 0:2, :, :].rearrange("p c q t -> p (c q t)"), 2 * P, "y_even", after_v2[:, 0 : 2 * P])
-        v01 = quantize(v01_grouped[:], 2 * P, "v01", after_v2[:, 2 * P : 4 * P])
-        odd3 = quantize(y_rest[:, 2, :, :].rearrange("p q t -> p (q t)"), P, "y3", after_v2[:, 4 * P : 5 * P])
-        y_mx = [
-            (even[0][:, 0:P], even[1][:, 0:P]),
-            (odd1[0][:], odd1[1][:]),
-            (even[0][:, P : 2 * P], even[1][:, P : 2 * P]),
-            (odd3[0], odd3[1][:]),
-        ]
+        after_v2 = sbuf([P, 4 * P], U32, "q_raw0")
+        v01 = quantize(v01_grouped[:], 2 * P, "v01", after_v2[:, 0 : 2 * P])
+        quantize_y(1, after_v2[:, 2 * P : 4 * P])
         out_rows = out[0].rearrange("(c p) e -> p c e", p=P)
-        early_sums = []
-        for h in range(2):
-            bank = psum.tile([P, 2, HALF], F32, name=f"bank{6 + h}")
-            for n in range(2):
-                second_product(bank[:, n, :], 2 * h + n, v01)
-            sums = sbuf([P, 2, HALF], F32, f"early_sums{h}")
-            nc.scalar.copy(out=sums[:], in_=bank[:])
-            early_sums.append(sums)
+
+        early_bank = psum.tile([P, 2, HALF], F32, name="bank6")
+        for c in range(2):
+            second_product(early_bank[:, c, :], c, v01)
+        early_sums = sbuf([P, 2, HALF], F32, "early_sums")
+        nc.scalar.copy(out=early_sums[:], in_=early_bank[:])
+        wide_banks = {c: psum.tile([P, 3 * P], F32, name=f"bank{c}") for c in (2, 3)}
+        for c in (2, 3):
+            second_product(wide_banks[c][:, 0:HALF], c, v01)
         bring_v(3)
         v2 = quantize(v_grouped[2], P, "v2", sbuf([P, P], U32, "ks_listed"))
-        late_banks = [psum.tile([P, 2, P], F32, name=f"bank{c}") for c in range(Q_TILES)]
-        for c in range(Q_TILES):
-            second_product(late_banks[c][:, 0, :], c, v2)
+        narrow_bank = psum.tile([P, 2, P], F32, name="bank7")
+        for c in range(2):
+            second_product(narrow_bank[:, c, :], c, v2)
+        for c in (2, 3):
+            second_product(wide_banks[c][:, HALF : 3 * P], c, v2)
 
-        def finish_early(h):
-            result = sbuf([P, 2, HALF], F32, f"early{h}")
-            nc.vector.tensor_tensor(out=result[:], in0=early_sums[h][:], in1=rs_sb[:, 2 * h : 2 * h + 2, 0:HALF], op=ALU.add)
-            nc.sync.dma_start(out=out_rows[:, 2 * h : 2 * h + 2, 0:HALF], in_=result[:])
-
-        finish_early(0)
-        v3 = quantize(v_grouped[3], P, "v3", sbuf([P, P], U32, "early_sums0"))
-        finish_early(1)
-        for c in range(Q_TILES):
-            second_product(late_banks[c][:, 1, :], c, v3)
-            late = sbuf([P, HALF], F32, f"late{c}")
-            nc.vector.tensor_tensor(
-                out=late[:], in0=late_banks[c][:].rearrange("p n e -> p (n e)"), in1=rs_sb[:, c, HALF:DV], op=ALU.add
-            )
-            nc.sync.dma_start(out=out[0, P * c : P * (c + 1), HALF:DV], in_=late[:])
+        low = sbuf([P, 2, 3 * P], F32, "low")
+        nc.vector.tensor_tensor(out=low[:, :, 0:HALF], in0=early_sums[:], in1=rs_sb[:, 0:2, 0:HALF], op=ALU.add)
+        nc.vector.tensor_tensor(out=low[:, :, HALF : 3 * P], in0=narrow_bank[:], in1=rs_sb[:, 0:2, HALF : 3 * P], op=ALU.add)
+        nc.sync.dma_start(out=out_rows[:, 0:2, 0 : 3 * P], in_=low[:])
+        v3 = quantize(v_grouped[3], P, "v3", sbuf([P, P], U32, "early_sums"))
+        for c in (2, 3):
+            wide = sbuf([P, 3 * P], F32, f"wide{c}")
+            nc.vector.tensor_tensor(out=wide[:], in0=wide_banks[c][:], in1=rs_sb[:, c, 0 : 3 * P], op=ALU.add)
+            nc.sync.dma_start(out=out_rows[:, c, 0 : 3 * P], in_=wide[:])
+        for h in range(2):
+            bank = psum.tile([P, 2, P], F32, name=f"bank{h}")
+            for n in range(2):
+                second_product(bank[:, n, :], 2 * h + n, v3)
+            last = sbuf([P, 2, P], F32, f"last{h}")
+            nc.vector.tensor_tensor(out=last[:], in0=bank[:], in1=rs_sb[:, 2 * h : 2 * h + 2, 3 * P : DV], op=ALU.add)
+            nc.sync.dma_start(out=out_rows[:, 2 * h : 2 * h + 2, 3 * P : DV], in_=last[:])

@@ -61,8 +61,9 @@ def tile_attend_mlp_relu2_topk_kernel(tc, qT, k_words, k_scales, vT, us, rs, off
                 out=ks_planes[32 * quad : 32 * quad + 4, :].bitcast(I32).rearrange("p (o n) -> p o n", o=PASSES),
                 in_=ks_dealt[96 + 8 * quad : 96 + 8 * (quad + 1), :].bitcast(I32),
             )
-        q_raw1 = sbuf([P, PACK, NQ], F32, "ks_listed")
-        nc.sync.dma_start(out=q_raw1[:], in_=q_rows[1])
+        q_raw1 = sbuf([P, 2, PACK, 2 * P], F32, "ks_listed")
+        for h in range(2):
+            nc.sync.dma_start(out=q_raw1[:, h, :, :], in_=q_rows[1, :, :, 2 * P * h : 2 * P * (h + 1)])
         kw_listed = sbuf([P, SLOTS], U32, "ks_pool")
         nc.vector.tensor_copy(kw_listed[:], kw_pool[:].bitcast(U32).indirect(offsets[:]))
         kw_dealt = sbuf([P, PASSES * SLOTS * 2], U8, "kw_dealt")
@@ -97,7 +98,7 @@ def tile_attend_mlp_relu2_topk_kernel(tc, qT, k_words, k_scales, vT, us, rs, off
                 q_mx[(0, 2 * h + n)] = (codes[:, P * n : P * (n + 1)], scales[:, P * n : P * (n + 1)])
 
         def round_q1(c, copy):
-            return round_q(q_raw1[:, :, P * c : P * (c + 1)], copy, f"q_grouped1_{c}")
+            return round_q(q_raw1[:, c // 2, :, P * (c % 2) : P * (c % 2 + 1)], copy, f"q_grouped1_{c}")
 
         def quantize_q1(c, grouped):
             codes, scales = quantize(grouped[:], P, f"q1_{c}")
@@ -106,10 +107,13 @@ def tile_attend_mlp_relu2_topk_kernel(tc, qT, k_words, k_scales, vT, us, rs, off
         q0_low = round_q(q_raw0[:, :, 0 : 2 * P], nc.vector.tensor_copy, "q_grouped0_0")
         q0_high = round_q(q_raw0[:, :, 2 * P : NQ], nc.scalar.copy, "q_grouped0_1")
         quantize_q0(0, q0_low)
-        quantize_q0(1, q0_high)
-        q1 = [round_q1(c, nc.scalar.copy if c % 2 else nc.vector.tensor_copy) for c in range(Q_TILES)]
-        for c in range(Q_TILES):
-            quantize_q1(c, q1[c])
+        q1 = [round_q1(0, nc.vector.tensor_copy), round_q1(1, nc.scalar.copy)]
+        quantize_q1(0, q1[0])
+        quantize_q1(1, q1[1])
+        quantize_q0(1, q0_high, sbuf([P, 2 * P], U32, "q_grouped1_1"))
+        q1.extend([round_q1(2, nc.vector.tensor_copy), round_q1(3, nc.vector.tensor_copy)])
+        quantize_q1(2, q1[2])
+        quantize_q1(3, q1[3])
 
         a_banks = [psum.tile([P, PACK, P], F32, name=f"bank{c}") for c in range(Q_TILES)]
         for c in range(Q_TILES):
@@ -194,27 +198,28 @@ def tile_attend_mlp_relu2_topk_kernel(tc, qT, k_words, k_scales, vT, us, rs, off
         rs_sb = sbuf([P, Q_TILES, DV], F32, "q_grouped1_3")
         for c in range(Q_TILES):
             nc.sync.dma_start(out=rs_sb[:, c, :], in_=rs[0, P * c : P * (c + 1), :])
-        y_grouped = [sbuf([P, 2, P, PACK], BF16, f"y_grouped{h}") for h in range(2)]
-        weigh_on_vector(0, scale_by_us(0), y_grouped[0][:, 0, :, :])
-        for c in range(1, Q_TILES):
-            weigh(square(c), y_grouped[c // 2][:, c % 2, :, :])
+        y_mx = []
+
+        def quantize_y(h, grouped, codes=None):
+            codes, scales = quantize(grouped[:].rearrange("p c q t -> p (c q t)"), 2 * P, f"y{h}", codes)
+            y_mx.extend([(codes[:, P * n : P * (n + 1)], scales[:, P * n : P * (n + 1)]) for n in range(2)])
+
+        y_low = sbuf([P, 2, P, PACK], BF16, "y_grouped")
+        for c in (0, 1):
+            weigh_on_vector(c, scale_by_us(c), y_low[:, c, :, :])
+        quantize_y(0, y_low)
+        y_high = sbuf([P, 2, P, PACK], BF16, "y_grouped")
+        for c in (2, 3):
+            weigh(square(c), y_high[:, c - 2, :, :])
         v01_grouped = sbuf([P, 2 * P * PACK], BF16, "relu1")
         v_grouped = [v01_grouped[:, 0 : P * PACK], v01_grouped[:, P * PACK : 2 * P * PACK]]
         for j in (2, 3):
             v_grouped.append(sbuf([P, P * PACK], BF16, f"v_grouped{j}")[:])
-        y_mx = []
-
-        def quantize_y(h, codes):
-            codes, scales = quantize(y_grouped[h][:].rearrange("p c q t -> p (c q t)"), 2 * P, f"y{h}", codes)
-            y_mx.extend([(codes[:, P * n : P * (n + 1)], scales[:, P * n : P * (n + 1)]) for n in range(2)])
-
-        bring_v(0)
-        bring_v(1)
-        quantize_y(0, sbuf([P, 2 * P], U32, "ks_pool"))
-        bring_v(2)
+        for j in range(3):
+            bring_v(j)
         after_v2 = sbuf([P, 4 * P], U32, "q_raw0")
         v01 = quantize(v01_grouped[:], 2 * P, "v01", after_v2[:, 0 : 2 * P])
-        quantize_y(1, after_v2[:, 2 * P : 4 * P])
+        quantize_y(1, y_high, after_v2[:, 2 * P : 4 * P])
         out_rows = out[0].rearrange("(c p) e -> p c e", p=P)
 
         early_bank = psum.tile([P, 2, HALF], F32, name="bank6")

@@ -222,35 +222,34 @@ def tile_attend_mlp_relu2_topk_kernel(tc, qT, k_words, k_scales, vT, us, rs, off
         quantize_y(1, y_high, after_v2[:, 2 * P : 4 * P])
         out_rows = out[0].rearrange("(c p) e -> p c e", p=P)
 
+        early_sums = sbuf([P, 2, HALF], F32, "early_sums")
         early_bank = psum.tile([P, 2, HALF], F32, name="bank6")
         for c in range(2):
             second_product(early_bank[:, c, :], c, v01)
-        early_sums = sbuf([P, 2, HALF], F32, "early_sums")
         nc.scalar.copy(out=early_sums[:], in_=early_bank[:])
-        wide_banks = {c: psum.tile([P, 3 * P], F32, name=f"bank{c}") for c in (2, 3)}
+        high_banks = {c: psum.tile([P, HALF], F32, name=f"bank{c}") for c in (2, 3)}
         for c in (2, 3):
-            second_product(wide_banks[c][:, 0:HALF], c, v01)
+            second_product(high_banks[c][:], c, v01)
         bring_v(3)
         v2 = quantize(v_grouped[2], P, "v2", sbuf([P, P], U32, "ks_listed"))
-        narrow_bank = psum.tile([P, 2, P], F32, name="bank7")
-        for c in range(2):
-            second_product(narrow_bank[:, c, :], c, v2)
-        for c in (2, 3):
-            second_product(wide_banks[c][:, HALF : 3 * P], c, v2)
+        bank2 = psum.tile([P, Q_TILES, P], F32, name="bank7")
+        for c in range(Q_TILES):
+            second_product(bank2[:, c, :], c, v2)
 
-        low = sbuf([P, 2, 3 * P], F32, "low")
-        nc.vector.tensor_tensor(out=low[:, :, 0:HALF], in0=early_sums[:], in1=rs_sb[:, 0:2, 0:HALF], op=ALU.add)
-        nc.vector.tensor_tensor(out=low[:, :, HALF : 3 * P], in0=narrow_bank[:], in1=rs_sb[:, 0:2, HALF : 3 * P], op=ALU.add)
-        nc.sync.dma_start(out=out_rows[:, 0:2, 0 : 3 * P], in_=low[:])
+        early = sbuf([P, 3, HALF], F32, "early")
+        nc.vector.tensor_tensor(out=early[:, 0:2, :], in0=early_sums[:], in1=rs_sb[:, 0:2, 0:HALF], op=ALU.add)
+        nc.vector.tensor_tensor(out=early[:, 2, :], in0=high_banks[2][:], in1=rs_sb[:, 2, 0:HALF], op=ALU.add)
+        nc.sync.dma_start(out=out_rows[:, 0:3, 0:HALF], in_=early[:])
         v3 = quantize(v_grouped[3], P, "v3", sbuf([P, P], U32, "early_sums"))
-        for c in (2, 3):
-            wide = sbuf([P, 3 * P], F32, f"wide{c}")
-            nc.vector.tensor_tensor(out=wide[:], in0=wide_banks[c][:], in1=rs_sb[:, c, 0 : 3 * P], op=ALU.add)
-            nc.sync.dma_start(out=out_rows[:, c, 0 : 3 * P], in_=wide[:])
-        for h in range(2):
-            bank = psum.tile([P, 2, P], F32, name=f"bank{h}")
+        early3 = sbuf([P, HALF], F32, "early3")
+        nc.vector.tensor_tensor(out=early3[:], in0=high_banks[3][:], in1=rs_sb[:, 3, 0:HALF], op=ALU.add)
+        nc.sync.dma_start(out=out_rows[:, 3, 0:HALF], in_=early3[:])
+        late = sbuf([P, Q_TILES, HALF], F32, "late")
+        nc.vector.tensor_tensor(out=late[:, :, 0:P], in0=bank2[:], in1=rs_sb[:, :, HALF : 3 * P], op=ALU.add)
+        for h in (1, 0):
+            pair = slice(2 * h, 2 * h + 2)
+            bank = psum.tile([P, 2, P], F32, name=("bank3", "bank1")[h])
             for n in range(2):
                 second_product(bank[:, n, :], 2 * h + n, v3)
-            last = sbuf([P, 2, P], F32, f"last{h}")
-            nc.vector.tensor_tensor(out=last[:], in0=bank[:], in1=rs_sb[:, 2 * h : 2 * h + 2, 3 * P : DV], op=ALU.add)
-            nc.sync.dma_start(out=out_rows[:, 2 * h : 2 * h + 2, 3 * P : DV], in_=last[:])
+            nc.vector.tensor_tensor(out=late[:, pair, P:HALF], in0=bank[:], in1=rs_sb[:, pair, 3 * P : DV], op=ALU.add)
+            nc.sync.dma_start(out=out_rows[:, pair, HALF:DV], in_=late[:, pair, :])

@@ -20,7 +20,8 @@ SLOTS, NEURONS, D, NQ, DV = 512, 2048, 1024, 512, 512
 PASSES = D // (P * PACK)
 Q_TILES = NQ // P
 E_BLOCKS = DV // P
-HALF = DV // 2
+EARLY = DV - P
+LIST_COLUMNS = SLOTS // 16
 
 FLOPS = 2 * SLOTS * NQ * (D + DV)
 
@@ -134,43 +135,25 @@ def tile_attend_mlp_relu2_topk_kernel(tc, qT, k_words, k_scales, vT, us, rs, off
         for j in range(E_BLOCKS):
             nc.sync.dma_start(out=v_pool[j][:], in_=vT[P * j : P * (j + 1), :])
 
-        def square(c):
-            relu = sbuf([P, P, PACK], F32, f"relu{c % 2}")
-            nc.scalar.activation(out=relu[:], in_=a_banks[c][:].rearrange("p t q -> p q t"), func=ACT.Relu)
-            squared = sbuf([P, P, PACK], F32, f"squared{c}")
-            nc.scalar.activation(out=squared[:], in_=relu[:], func=ACT.Square)
-            return squared
+        rs_sb = sbuf([P, Q_TILES, DV], F32, "q_grouped1_3")
+        for c in range(Q_TILES):
+            nc.sync.dma_start(out=rs_sb[:, c, :], in_=rs[0, P * c : P * (c + 1), :])
 
-        def weigh(squared, grouped):
-            nc.gpsimd.tensor_tensor(
-                out=grouped,
-                in0=squared[:],
-                in1=us_cols[:].unsqueeze(1).to_broadcast([P, P, PACK]),
-                op=ALU.mult,
-            )
-
-        def scale_by_us(c):
-            scaled = sbuf([P, PACK, P], F32, f"scaled{c}")
-            for t in range(PACK):
-                nc.scalar.activation(out=scaled[:, t, :], in_=a_banks[c][:, t, :], func=ACT.Copy, scale=us_cols[:, t : t + 1])
-            return scaled
-
-        def weigh_on_vector(c, scaled, grouped):
-            nc.vector.scalar_tensor_tensor(
-                out=grouped,
-                in0=a_banks[c][:].rearrange("p t q -> p q t"),
-                scalar=0.0,
-                in1=scaled[:].rearrange("p t q -> p q t"),
-                op0=ALU.max,
-                op1=ALU.mult,
-            )
-
-        def gather_v(j):
+        def gather_v(j, vector_columns):
             listed = sbuf([P, SLOTS], BF16, f"v_listed{j}")
-            nc.vector.tensor_copy(listed[:], v_pool[j][:].indirect(offsets[:]))
+            cut = 16 * vector_columns
+            if vector_columns > 0:
+                nc.vector.tensor_copy(listed[:, 0:cut], v_pool[j][:].indirect(offsets[:, 0:vector_columns]))
+            if vector_columns < LIST_COLUMNS:
+                nc.scalar.activation(
+                    out=listed[:, cut:SLOTS],
+                    in_=v_pool[j][:].indirect(offsets[:, vector_columns:LIST_COLUMNS]),
+                    func=ACT.Copy,
+                )
             return listed
 
-        def turn_v(listed, turned, grouped):
+        def turn_v(j, listed, grouped):
+            turned = psum.tile([P, 2, P], F32, name=f"bank{4 + j % 2}")
             words = listed[:].bitcast(F32)
             for u in range(2):
                 nc.tensor.transpose(turned[:, u, :], words[:, u : 2 * P : 2], ident[:])
@@ -180,76 +163,87 @@ def tile_attend_mlp_relu2_topk_kernel(tc, qT, k_words, k_scales, vT, us, rs, off
             )
 
         def second_product(acc, c, v_mx):
-            y_codes, y_scales = y_mx[c]
+            tile_codes, tile_scales = y_mx[c]
             nc.tensor.matmul_mx(
                 out=acc,
-                lhsT=y_codes.bitcast(FP8X4),
-                lhsT_scale=y_scales,
+                lhsT=tile_codes.bitcast(FP8X4),
+                lhsT_scale=tile_scales,
                 rhs=v_mx[0][:].bitcast(FP8X4),
                 rhs_scale=v_mx[1][:],
                 start=True,
                 stop=True,
             )
 
-        def bring_v(j):
-            turned = psum.tile([P, 2, P], F32, name=f"bank{4 + j % 2}")
-            turn_v(gather_v(j), turned, v_grouped[j])
+        us_along_q = us_cols[:].unsqueeze(1).to_broadcast([P, P, PACK])
+        y_grouped = sbuf([P, Q_TILES, P, PACK], BF16, "y_grouped")
 
-        rs_sb = sbuf([P, Q_TILES, DV], F32, "q_grouped1_3")
-        for c in range(Q_TILES):
-            nc.sync.dma_start(out=rs_sb[:, c, :], in_=rs[0, P * c : P * (c + 1), :])
-        y_mx = []
+        def weigh_on_vector(c, name):
+            scores = a_banks[c][:].rearrange("p t q -> p q t")
+            weighed = sbuf([P, P, PACK], F32, name)
+            nc.vector.scalar_tensor_tensor(
+                out=weighed[:], in0=scores, scalar=0.0, in1=us_along_q, op0=ALU.max, op1=ALU.mult
+            )
+            nc.vector.tensor_tensor(out=y_grouped[:, c, :, :], in0=scores, in1=weighed[:], op=ALU.mult)
 
-        def quantize_y(h, grouped, codes=None):
-            codes, scales = quantize(grouped[:].rearrange("p c q t -> p (c q t)"), 2 * P, f"y{h}", codes)
-            y_mx.extend([(codes[:, P * n : P * (n + 1)], scales[:, P * n : P * (n + 1)]) for n in range(2)])
+        def weigh_on_gpsimd(c):
+            scores = a_banks[c][:].rearrange("p t q -> p q t")
+            squared = sbuf([P, P, PACK], F32, f"squared{c}")
+            halves = [slice(0, P // 2), slice(P // 2, P)]
+            relus = [sbuf([P, P // 2, PACK], F32, f"relu{h}") for h in range(2)]
+            for relu, half in zip(relus, halves):
+                nc.scalar.activation(out=relu[:], in_=scores[:, half, :], func=ACT.Relu)
+            for relu, half in zip(relus, halves):
+                nc.scalar.activation(out=squared[:, half, :], in_=relu[:], func=ACT.Square)
+            nc.gpsimd.tensor_tensor(out=y_grouped[:, c, :, :], in0=squared[:], in1=us_along_q, op=ALU.mult)
 
-        y_low = sbuf([P, 2, P, PACK], BF16, "y_grouped")
-        for c in (0, 1):
-            weigh_on_vector(c, scale_by_us(c), y_low[:, c, :, :])
-        quantize_y(0, y_low)
-        y_high = sbuf([P, 2, P, PACK], BF16, "y_grouped")
-        for c in (2, 3):
-            weigh(square(c), y_high[:, c - 2, :, :])
-        v01_grouped = sbuf([P, 2 * P * PACK], BF16, "relu1")
-        v_grouped = [v01_grouped[:, 0 : P * PACK], v01_grouped[:, P * PACK : 2 * P * PACK]]
-        for j in (2, 3):
-            v_grouped.append(sbuf([P, P * PACK], BF16, f"v_grouped{j}")[:])
-        for j in range(3):
-            bring_v(j)
-        after_v2 = sbuf([P, 4 * P], U32, "q_raw0")
-        v01 = quantize(v01_grouped[:], 2 * P, "v01", after_v2[:, 0 : 2 * P])
-        quantize_y(1, y_high, after_v2[:, 2 * P : 4 * P])
+        weigh_on_vector(0, "weighed0")
+        weigh_on_gpsimd(1)
+        weigh_on_gpsimd(2)
+        listed = [gather_v(0, LIST_COLUMNS)]
+        weigh_on_vector(3, "kw_pool")
+        y_codes, y_scales = quantize(y_grouped[:].rearrange("p c q t -> p (c q t)"), NQ, "y")
+        y_mx = [(y_codes[:, P * c : P * (c + 1)], y_scales[:, P * c : P * (c + 1)]) for c in range(Q_TILES)]
+
+        early_banks = [psum.tile([P, EARLY], F32, name=f"bank{c}") for c in range(Q_TILES)]
+
+        def multiply_early(j, grouped):
+            v_mx = quantize(grouped[:], P, f"v{j}")
+            for c in range(Q_TILES):
+                second_product(early_banks[c][:, P * j : P * (j + 1)], c, v_mx)
+
+        listed.append(gather_v(1, 0))
+        v0_grouped = sbuf([P, P * PACK], BF16, "ks_pool")
+        turn_v(0, listed[0], v0_grouped[:])
+        multiply_early(0, v0_grouped)
+        listed.append(gather_v(2, 16))
+        v1_grouped = sbuf([P, P * PACK], BF16, "q_raw0")
+        turn_v(1, listed[1], v1_grouped[:])
+        v2_grouped = sbuf([P, P * PACK], BF16, "v2_grouped")
+        turn_v(2, listed[2], v2_grouped[:])
+        multiply_early(1, v1_grouped)
+        multiply_early(2, v2_grouped)
+        listed.append(gather_v(3, 12))
+        v3_grouped = sbuf([P, P * PACK], BF16, "v3_grouped")
+        turn_v(3, listed[3], v3_grouped[:])
+
         out_rows = out[0].rearrange("(c p) e -> p c e", p=P)
 
-        early_sums = sbuf([P, 2, HALF], F32, "early_sums")
-        early_bank = psum.tile([P, 2, HALF], F32, name="bank6")
-        for c in range(2):
-            second_product(early_bank[:, c, :], c, v01)
-        nc.scalar.copy(out=early_sums[:], in_=early_bank[:])
-        high_banks = {c: psum.tile([P, HALF], F32, name=f"bank{c}") for c in (2, 3)}
-        for c in (2, 3):
-            second_product(high_banks[c][:], c, v01)
-        bring_v(3)
-        v2 = quantize(v_grouped[2], P, "v2", sbuf([P, P], U32, "ks_listed"))
-        bank2 = psum.tile([P, Q_TILES, P], F32, name="bank7")
-        for c in range(Q_TILES):
-            second_product(bank2[:, c, :], c, v2)
+        early = sbuf([P, Q_TILES, EARLY], F32, "ks_listed")
 
-        early = sbuf([P, 3, HALF], F32, "early")
-        nc.vector.tensor_tensor(out=early[:, 0:2, :], in0=early_sums[:], in1=rs_sb[:, 0:2, 0:HALF], op=ALU.add)
-        nc.vector.tensor_tensor(out=early[:, 2, :], in0=high_banks[2][:], in1=rs_sb[:, 2, 0:HALF], op=ALU.add)
-        nc.sync.dma_start(out=out_rows[:, 0:3, 0:HALF], in_=early[:])
-        v3 = quantize(v_grouped[3], P, "v3", sbuf([P, P], U32, "early_sums"))
-        early3 = sbuf([P, HALF], F32, "early3")
-        nc.vector.tensor_tensor(out=early3[:], in0=high_banks[3][:], in1=rs_sb[:, 3, 0:HALF], op=ALU.add)
-        nc.sync.dma_start(out=out_rows[:, 3, 0:HALF], in_=early3[:])
-        late = sbuf([P, Q_TILES, HALF], F32, "late")
-        nc.vector.tensor_tensor(out=late[:, :, 0:P], in0=bank2[:], in1=rs_sb[:, :, HALF : 3 * P], op=ALU.add)
-        for h in (1, 0):
+        def finish_early(c):
+            nc.vector.tensor_tensor(out=early[:, c, :], in0=early_banks[c][:], in1=rs_sb[:, c, 0:EARLY], op=ALU.add)
+            nc.sync.dma_start(out=out_rows[:, c, 0:EARLY], in_=early[:, c, :])
+
+        finish_early(0)
+        finish_early(1)
+        v3 = quantize(v3_grouped[:], P, "v3")
+        finish_early(2)
+        finish_early(3)
+        for h in range(2):
             pair = slice(2 * h, 2 * h + 2)
-            bank = psum.tile([P, 2, P], F32, name=("bank3", "bank1")[h])
+            bank = psum.tile([P, 2, P], F32, name=f"bank{6 + h}")
             for n in range(2):
                 second_product(bank[:, n, :], 2 * h + n, v3)
-            nc.vector.tensor_tensor(out=late[:, pair, P:HALF], in0=bank[:], in1=rs_sb[:, pair, 3 * P : DV], op=ALU.add)
-            nc.sync.dma_start(out=out_rows[:, pair, HALF:DV], in_=late[:, pair, :])
+            late = sbuf([P, 2, P], F32, f"late{h}")
+            nc.vector.tensor_tensor(out=late[:], in0=bank[:], in1=rs_sb[:, pair, EARLY:DV], op=ALU.add)
+            nc.sync.dma_start(out=out_rows[:, pair, EARLY:DV], in_=late[:])

@@ -20,7 +20,7 @@ SLOTS, NEURONS, D, NQ, DV = 512, 2048, 1024, 512, 512
 PASSES = D // (P * PACK)
 Q_TILES = NQ // P
 E_BLOCKS = DV // P
-EARLY = DV - P
+HALF = DV // 2
 LIST_COLUMNS = SLOTS // 16
 
 FLOPS = 2 * SLOTS * NQ * (D + DV)
@@ -135,9 +135,14 @@ def tile_attend_mlp_relu2_topk_kernel(tc, qT, k_words, k_scales, vT, us, rs, off
         for j in range(E_BLOCKS):
             nc.sync.dma_start(out=v_pool[j][:], in_=vT[P * j : P * (j + 1), :])
 
-        rs_sb = sbuf([P, Q_TILES, DV], F32, "q_grouped1_3")
-        for c in range(Q_TILES):
-            nc.sync.dma_start(out=rs_sb[:, c, :], in_=rs[0, P * c : P * (c + 1), :])
+        rs_rows = rs[0].rearrange("(c p) e -> p c e", p=P)
+        pairs = [slice(0, 2), slice(2, 4)]
+        rs_early = [sbuf([P, 2, HALF], F32, name) for name in ("q_grouped1_3", "q1_2_codes")]
+        rs_late = sbuf([P, Q_TILES, HALF], F32, "q1_3_codes")
+        for h in range(2):
+            nc.sync.dma_start(out=rs_early[h][:], in_=rs_rows[:, pairs[h], 0:HALF])
+        for pair in pairs:
+            nc.sync.dma_start(out=rs_late[:, pair, :], in_=rs_rows[:, pair, HALF:DV])
 
         def gather_v(j, vector_columns):
             listed = sbuf([P, SLOTS], BF16, f"v_listed{j}")
@@ -204,12 +209,12 @@ def tile_attend_mlp_relu2_topk_kernel(tc, qT, k_words, k_scales, vT, us, rs, off
         y_codes, y_scales = quantize(y_grouped[:].rearrange("p c q t -> p (c q t)"), NQ, "y")
         y_mx = [(y_codes[:, P * c : P * (c + 1)], y_scales[:, P * c : P * (c + 1)]) for c in range(Q_TILES)]
 
-        early_banks = [psum.tile([P, EARLY], F32, name=f"bank{c}") for c in range(Q_TILES)]
+        early_banks = [psum.tile([P, 2, HALF], F32, name=f"bank{2 * h}") for h in range(2)]
 
         def multiply_early(j, grouped):
             v_mx = quantize(grouped[:], P, f"v{j}")
             for c in range(Q_TILES):
-                second_product(early_banks[c][:, P * j : P * (j + 1)], c, v_mx)
+                second_product(early_banks[c // 2][:, c % 2, P * j : P * (j + 1)], c, v_mx)
 
         listed.append(gather_v(1, 0))
         v0_grouped = sbuf([P, P * PACK], BF16, "ks_pool")
@@ -218,32 +223,30 @@ def tile_attend_mlp_relu2_topk_kernel(tc, qT, k_words, k_scales, vT, us, rs, off
         listed.append(gather_v(2, 16))
         v1_grouped = sbuf([P, P * PACK], BF16, "q_raw0")
         turn_v(1, listed[1], v1_grouped[:])
-        v2_grouped = sbuf([P, P * PACK], BF16, "v2_grouped")
-        turn_v(2, listed[2], v2_grouped[:])
         multiply_early(1, v1_grouped)
-        multiply_early(2, v2_grouped)
-        listed.append(gather_v(3, 12))
+        listed.append(gather_v(3, 16))
+        v2_grouped = sbuf([P, P * PACK], BF16, "ks_listed")
+        turn_v(2, listed[2], v2_grouped[:])
         v3_grouped = sbuf([P, P * PACK], BF16, "v3_grouped")
         turn_v(3, listed[3], v3_grouped[:])
 
         out_rows = out[0].rearrange("(c p) e -> p c e", p=P)
 
-        early = sbuf([P, Q_TILES, EARLY], F32, "ks_listed")
+        def finish(bank, residual, tiles, columns, name):
+            result = sbuf(list(bank.shape), F32, name)
+            nc.vector.tensor_tensor(out=result[:], in0=bank, in1=residual, op=ALU.add)
+            nc.sync.dma_start(out=out_rows[:, tiles, columns], in_=result[:])
 
-        def finish_early(c):
-            nc.vector.tensor_tensor(out=early[:, c, :], in0=early_banks[c][:], in1=rs_sb[:, c, 0:EARLY], op=ALU.add)
-            nc.sync.dma_start(out=out_rows[:, c, 0:EARLY], in_=early[:, c, :])
-
-        finish_early(0)
-        finish_early(1)
-        v3 = quantize(v3_grouped[:], P, "v3")
-        finish_early(2)
-        finish_early(3)
+        finish(early_banks[0][:], rs_early[0][:], pairs[0], slice(0, HALF), "early0")
+        v2 = quantize(v2_grouped[:], P, "v2")
+        bank2 = psum.tile([P, Q_TILES, P], F32, name="bank1")
+        for c in range(Q_TILES):
+            second_product(bank2[:, c, :], c, v2)
+        finish(early_banks[1][:], rs_early[1][:], pairs[1], slice(0, HALF), "early1")
+        v3 = quantize(v3_grouped[:], P, "v3", sbuf([P, P], U32, "q1_2_codes"))
+        finish(bank2[:], rs_late[:, :, 0:P], slice(0, Q_TILES), slice(HALF, 3 * P), "middle")
         for h in range(2):
-            pair = slice(2 * h, 2 * h + 2)
             bank = psum.tile([P, 2, P], F32, name=f"bank{6 + h}")
             for n in range(2):
                 second_product(bank[:, n, :], 2 * h + n, v3)
-            late = sbuf([P, 2, P], F32, f"late{h}")
-            nc.vector.tensor_tensor(out=late[:], in0=bank[:], in1=rs_sb[:, pair, EARLY:DV], op=ALU.add)
-            nc.sync.dma_start(out=out_rows[:, pair, EARLY:DV], in_=late[:])
+            finish(bank[:], rs_late[:, pairs[h], P:HALF], pairs[h], slice(3 * P, DV), f"late{h}")

@@ -141,8 +141,7 @@ def tile_attend_mlp_relu2_topk_kernel(tc, qT, k_words, k_scales, vT, us, rs, off
         rs_late = sbuf([P, Q_TILES, HALF], F32, "q1_3_codes")
         for h in range(2):
             nc.sync.dma_start(out=rs_early[h][:], in_=rs_rows[:, pairs[h], 0:HALF])
-        for pair in pairs:
-            nc.sync.dma_start(out=rs_late[:, pair, :], in_=rs_rows[:, pair, HALF:DV])
+        nc.sync.dma_start(out=rs_late[:], in_=rs_rows[:, :, HALF:DV])
 
         def gather_v(j, vector_columns):
             listed = sbuf([P, SLOTS], BF16, f"v_listed{j}")
@@ -209,24 +208,27 @@ def tile_attend_mlp_relu2_topk_kernel(tc, qT, k_words, k_scales, vT, us, rs, off
         y_codes, y_scales = quantize(y_grouped[:].rearrange("p c q t -> p (c q t)"), NQ, "y")
         y_mx = [(y_codes[:, P * c : P * (c + 1)], y_scales[:, P * c : P * (c + 1)]) for c in range(Q_TILES)]
 
-        early_banks = [psum.tile([P, 2, HALF], F32, name=f"bank{2 * h}") for h in range(2)]
+        v01_codes = sbuf([P, HALF], U32, "v01_codes")
+        v01_scales = sbuf([P, HALF], U8, "v01_scales")
 
-        def multiply_early(j, grouped):
-            v_mx = quantize(grouped[:], P, f"v{j}")
-            for c in range(Q_TILES):
-                second_product(early_banks[c // 2][:, c % 2, P * j : P * (j + 1)], c, v_mx)
+        def quantize_early(j, grouped):
+            columns = slice(P * j, P * (j + 1))
+            nc.vector.quantize_mx(out=v01_codes[:, columns].bitcast(FP8X4), scales=v01_scales[:, columns], in_=grouped[:])
 
         listed.append(gather_v(1, 0))
         v0_grouped = sbuf([P, P * PACK], BF16, "ks_pool")
         turn_v(0, listed[0], v0_grouped[:])
-        multiply_early(0, v0_grouped)
+        quantize_early(0, v0_grouped)
         listed.append(gather_v(2, 16))
         v1_grouped = sbuf([P, P * PACK], BF16, "q_raw0")
         turn_v(1, listed[1], v1_grouped[:])
-        multiply_early(1, v1_grouped)
-        listed.append(gather_v(3, 16))
-        v2_grouped = sbuf([P, P * PACK], BF16, "ks_listed")
+        v2_grouped = sbuf([P, P * PACK], BF16, "v2_grouped")
         turn_v(2, listed[2], v2_grouped[:])
+        quantize_early(1, v1_grouped)
+        early_banks = [psum.tile([P, 2, HALF], F32, name=f"bank{2 * h}") for h in range(2)]
+        for c in range(Q_TILES):
+            second_product(early_banks[c // 2][:, c % 2, :], c, (v01_codes, v01_scales))
+        listed.append(gather_v(3, 16))
         v3_grouped = sbuf([P, P * PACK], BF16, "v3_grouped")
         turn_v(3, listed[3], v3_grouped[:])
 
@@ -238,15 +240,14 @@ def tile_attend_mlp_relu2_topk_kernel(tc, qT, k_words, k_scales, vT, us, rs, off
             nc.sync.dma_start(out=out_rows[:, tiles, columns], in_=result[:])
 
         finish(early_banks[0][:], rs_early[0][:], pairs[0], slice(0, HALF), "early0")
-        v2 = quantize(v2_grouped[:], P, "v2")
+        v2 = quantize(v2_grouped[:], P, "v2", sbuf([P, P], U32, "ks_listed"))
         bank2 = psum.tile([P, Q_TILES, P], F32, name="bank1")
         for c in range(Q_TILES):
             second_product(bank2[:, c, :], c, v2)
         finish(early_banks[1][:], rs_early[1][:], pairs[1], slice(0, HALF), "early1")
-        v3 = quantize(v3_grouped[:], P, "v3", sbuf([P, P], U32, "q1_2_codes"))
+        v3 = quantize(v3_grouped[:], P, "v3", sbuf([P, P], U32, "q_grouped1_3"))
         finish(bank2[:], rs_late[:, :, 0:P], slice(0, Q_TILES), slice(HALF, 3 * P), "middle")
-        for h in range(2):
-            bank = psum.tile([P, 2, P], F32, name=f"bank{6 + h}")
-            for n in range(2):
-                second_product(bank[:, n, :], 2 * h + n, v3)
-            finish(bank[:], rs_late[:, pairs[h], P:HALF], pairs[h], slice(3 * P, DV), f"late{h}")
+        bank3 = psum.tile([P, Q_TILES, P], F32, name="bank6")
+        for c in range(Q_TILES):
+            second_product(bank3[:, c, :], c, v3)
+        finish(bank3[:], rs_late[:, :, P:HALF], slice(0, Q_TILES), slice(3 * P, DV), "late")

@@ -32,7 +32,12 @@ def tile_attend_mlp_relu2_topk_kernel(tc, qT, k_words, k_scales, vT, us, rs, off
         keep = ctx.enter_context(tc.tile_pool(name="keep", bufs=1))
         psum = ctx.enter_context(tc.psum_pool(name="psum", bufs=1))
 
+        shared = ctx.enter_context(tc.tile_pool(name="shared", bufs=1))
+        places = {"q_raw0": 0, "v_pool2": 0, "v1_grouped": 0, "v01_codes": 1024, "y0_codes": 2048, "y1_codes": 0}
+
         def sbuf(shape, dtype, name):
+            if name in places:
+                return shared.tile(shape, dtype, name=name, align_bytes=64, offset=places[name])
             return keep.tile(shape, dtype, name=name, align_bytes=64)
 
         offsets = keep.tile([P, SLOTS // 16], U16, name="offsets")
@@ -62,9 +67,8 @@ def tile_attend_mlp_relu2_topk_kernel(tc, qT, k_words, k_scales, vT, us, rs, off
                 out=ks_planes[32 * quad : 32 * quad + 4, :].bitcast(I32).rearrange("p (o n) -> p o n", o=PASSES),
                 in_=ks_dealt[96 + 8 * quad : 96 + 8 * (quad + 1), :].bitcast(I32),
             )
-        q_raw1 = sbuf([P, 2, PACK, 2 * P], F32, "ks_listed")
-        for h in range(2):
-            nc.sync.dma_start(out=q_raw1[:, h, :, :], in_=q_rows[1, :, :, 2 * P * h : 2 * P * (h + 1)])
+        q_raw1 = sbuf([P, PACK, NQ], F32, "ks_listed")
+        nc.sync.dma_start(out=q_raw1[:], in_=q_rows[1])
         kw_listed = sbuf([P, SLOTS], U32, "ks_pool")
         nc.vector.tensor_copy(kw_listed[:], kw_pool[:].bitcast(U32).indirect(offsets[:]))
         kw_dealt = sbuf([P, PASSES * SLOTS * 2], U8, "kw_dealt")
@@ -99,7 +103,7 @@ def tile_attend_mlp_relu2_topk_kernel(tc, qT, k_words, k_scales, vT, us, rs, off
                 q_mx[(0, 2 * h + n)] = (codes[:, P * n : P * (n + 1)], scales[:, P * n : P * (n + 1)])
 
         def round_q1(c, copy):
-            return round_q(q_raw1[:, c // 2, :, P * (c % 2) : P * (c % 2 + 1)], copy, f"q_grouped1_{c}")
+            return round_q(q_raw1[:, :, P * c : P * (c + 1)], copy, f"q_grouped1_{c}")
 
         def quantize_q1(c, grouped):
             codes, scales = quantize(grouped[:], P, f"q1_{c}")
@@ -108,13 +112,10 @@ def tile_attend_mlp_relu2_topk_kernel(tc, qT, k_words, k_scales, vT, us, rs, off
         q0_low = round_q(q_raw0[:, :, 0 : 2 * P], nc.vector.tensor_copy, "q_grouped0_0")
         q0_high = round_q(q_raw0[:, :, 2 * P : NQ], nc.scalar.copy, "q_grouped0_1")
         quantize_q0(0, q0_low)
-        q1 = [round_q1(0, nc.vector.tensor_copy), round_q1(1, nc.scalar.copy)]
-        quantize_q1(0, q1[0])
-        quantize_q1(1, q1[1])
-        quantize_q0(1, q0_high, sbuf([P, 2 * P], U32, "q_grouped1_1"))
-        q1.extend([round_q1(2, nc.vector.tensor_copy), round_q1(3, nc.vector.tensor_copy)])
-        quantize_q1(2, q1[2])
-        quantize_q1(3, q1[3])
+        quantize_q0(1, q0_high)
+        q1 = [round_q1(c, (nc.vector.tensor_copy, nc.scalar.copy)[c % 2]) for c in range(Q_TILES)]
+        for c in range(Q_TILES):
+            quantize_q1(c, q1[c])
 
         a_banks = [psum.tile([P, PACK, P], F32, name=f"bank{c}") for c in range(Q_TILES)]
         for c in range(Q_TILES):
@@ -131,17 +132,15 @@ def tile_attend_mlp_relu2_topk_kernel(tc, qT, k_words, k_scales, vT, us, rs, off
                         stop=(o == PASSES - 1 and t == PACK - 1),
                     )
 
-        v_pool = [sbuf([P, NEURONS], F32, name) for name in ("kw_pool", "ks_pool", "q_raw0", "ks_listed")]
+        v_pool = [sbuf([P, NEURONS], F32, name) for name in ("kw_pool", "ks_pool", "v_pool2", "ks_listed")]
         for j in range(E_BLOCKS):
             nc.sync.dma_start(out=v_pool[j][:], in_=vT[P * j : P * (j + 1), :])
 
         rs_rows = rs[0].rearrange("(c p) e -> p c e", p=P)
         pairs = [slice(0, 2), slice(2, 4)]
-        rs_early = [sbuf([P, 2, HALF], F32, name) for name in ("q_grouped1_3", "q1_2_codes")]
-        rs_late = sbuf([P, Q_TILES, HALF], F32, "q1_3_codes")
-        for h in range(2):
-            nc.sync.dma_start(out=rs_early[h][:], in_=rs_rows[:, pairs[h], 0:HALF])
-        nc.sync.dma_start(out=rs_late[:], in_=rs_rows[:, :, HALF:DV])
+        rs_sb = sbuf([P, Q_TILES, DV], F32, "q_grouped1_3")
+        for pair in pairs:
+            nc.sync.dma_start(out=rs_sb[:, pair, :], in_=rs_rows[:, pair, :])
 
         def gather_v(j, vector_columns):
             listed = sbuf([P, SLOTS], BF16, f"v_listed{j}")
@@ -200,31 +199,35 @@ def tile_attend_mlp_relu2_topk_kernel(tc, qT, k_words, k_scales, vT, us, rs, off
                 nc.scalar.activation(out=squared[:, half, :], in_=relu[:], func=ACT.Square)
             nc.gpsimd.tensor_tensor(out=y_grouped[:, c, :, :], in0=squared[:], in1=us_along_q, op=ALU.mult)
 
-        weigh_on_vector(0, "weighed0")
-        weigh_on_gpsimd(1)
+        weigh_on_gpsimd(0)
+        weigh_on_vector(1, "weighed1")
         weigh_on_gpsimd(2)
-        listed = [gather_v(0, LIST_COLUMNS)]
-        weigh_on_vector(3, "kw_pool")
-        y_codes, y_scales = quantize(y_grouped[:].rearrange("p c q t -> p (c q t)"), NQ, "y")
-        y_mx = [(y_codes[:, P * c : P * (c + 1)], y_scales[:, P * c : P * (c + 1)]) for c in range(Q_TILES)]
+        weigh_on_gpsimd(3)
+        listed = [gather_v(j, LIST_COLUMNS) for j in range(2)]
+        v0_grouped = sbuf([P, P * PACK], BF16, "relu1")
+        turn_v(0, listed[0], v0_grouped[:])
+        listed.append(gather_v(2, 16))
+        y_mx = []
 
-        v01_codes = sbuf([P, HALF], U32, "v01_codes")
-        v01_scales = sbuf([P, HALF], U8, "v01_scales")
+        def quantize_y(h):
+            codes, scales = quantize(y_grouped[:, pairs[h], :, :].rearrange("p c q t -> p (c q t)"), 2 * P, f"y{h}")
+            y_mx.extend([(codes[:, P * n : P * (n + 1)], scales[:, P * n : P * (n + 1)]) for n in range(2)])
+
+        quantize_y(0)
 
         def quantize_early(j, grouped):
             columns = slice(P * j, P * (j + 1))
             nc.vector.quantize_mx(out=v01_codes[:, columns].bitcast(FP8X4), scales=v01_scales[:, columns], in_=grouped[:])
 
-        listed.append(gather_v(1, 0))
-        v0_grouped = sbuf([P, P * PACK], BF16, "ks_pool")
-        turn_v(0, listed[0], v0_grouped[:])
+        v01_codes = sbuf([P, HALF], U32, "v01_codes")
+        v01_scales = sbuf([P, HALF], U8, "v01_scales")
         quantize_early(0, v0_grouped)
-        listed.append(gather_v(2, 16))
-        v1_grouped = sbuf([P, P * PACK], BF16, "q_raw0")
+        v1_grouped = sbuf([P, P * PACK], BF16, "v1_grouped")
         turn_v(1, listed[1], v1_grouped[:])
         v2_grouped = sbuf([P, P * PACK], BF16, "v2_grouped")
         turn_v(2, listed[2], v2_grouped[:])
         quantize_early(1, v1_grouped)
+        quantize_y(1)
         early_banks = [psum.tile([P, 2, HALF], F32, name=f"bank{2 * h}") for h in range(2)]
         for c in range(Q_TILES):
             second_product(early_banks[c // 2][:, c % 2, :], c, (v01_codes, v01_scales))
@@ -234,20 +237,21 @@ def tile_attend_mlp_relu2_topk_kernel(tc, qT, k_words, k_scales, vT, us, rs, off
 
         out_rows = out[0].rearrange("(c p) e -> p c e", p=P)
 
-        def finish(bank, residual, tiles, columns, name):
+        def finish(bank, tiles, columns, name):
             result = sbuf(list(bank.shape), F32, name)
-            nc.vector.tensor_tensor(out=result[:], in0=bank, in1=residual, op=ALU.add)
+            nc.vector.tensor_tensor(out=result[:], in0=bank, in1=rs_sb[:, tiles, columns], op=ALU.add)
             nc.sync.dma_start(out=out_rows[:, tiles, columns], in_=result[:])
 
-        finish(early_banks[0][:], rs_early[0][:], pairs[0], slice(0, HALF), "early0")
         v2 = quantize(v2_grouped[:], P, "v2", sbuf([P, P], U32, "ks_listed"))
-        bank2 = psum.tile([P, Q_TILES, P], F32, name="bank1")
+        banks2 = [psum.tile([P, 2, P], F32, name=name) for name in ("bank1", "bank3")]
         for c in range(Q_TILES):
-            second_product(bank2[:, c, :], c, v2)
-        finish(early_banks[1][:], rs_early[1][:], pairs[1], slice(0, HALF), "early1")
-        v3 = quantize(v3_grouped[:], P, "v3", sbuf([P, P], U32, "q_grouped1_3"))
-        finish(bank2[:], rs_late[:, :, 0:P], slice(0, Q_TILES), slice(HALF, 3 * P), "middle")
+            second_product(banks2[c // 2][:, c % 2, :], c, v2)
+        finish(early_banks[0][:], pairs[0], slice(0, HALF), "early0")
+        finish(banks2[0][:], pairs[0], slice(HALF, 3 * P), "middle0")
+        v3 = quantize(v3_grouped[:], P, "v3")
+        finish(early_banks[1][:], pairs[1], slice(0, HALF), "early1")
+        finish(banks2[1][:], pairs[1], slice(HALF, 3 * P), "middle1")
         bank3 = psum.tile([P, Q_TILES, P], F32, name="bank6")
         for c in range(Q_TILES):
             second_product(bank3[:, c, :], c, v3)
-        finish(bank3[:], rs_late[:, :, P:HALF], slice(0, Q_TILES), slice(3 * P, DV), "late")
+        finish(bank3[:], slice(0, Q_TILES), slice(3 * P, DV), "late")

@@ -20,8 +20,10 @@ SLOTS, NEURONS, D, NQ, DV = 512, 2048, 1024, 512, 512
 PASSES = D // (P * PACK)
 Q_TILES = NQ // P
 E_BLOCKS = DV // P
-HALF = DV // 2
+EARLY = DV - P
 LIST_COLUMNS = SLOTS // 16
+ROOM = 4 * NEURONS
+VECTOR_COLUMNS = (14, 14, 16, 14)
 
 FLOPS = 2 * SLOTS * NQ * (D + DV)
 
@@ -31,16 +33,37 @@ def tile_attend_mlp_relu2_topk_kernel(tc, qT, k_words, k_scales, vT, us, rs, off
     with ExitStack() as ctx:
         keep = ctx.enter_context(tc.tile_pool(name="keep", bufs=1))
         psum = ctx.enter_context(tc.psum_pool(name="psum", bufs=1))
-
         shared = ctx.enter_context(tc.tile_pool(name="shared", bufs=1))
-        places = {"q_raw0": 0, "v_pool2": 0, "v1_grouped": 0, "v01_codes": 1024, "y0_codes": 2048, "y1_codes": 0}
+        places = {
+            "kw_pool": 0,
+            "v_pool0": 0,
+            "ks_pool": ROOM,
+            "kw_listed": ROOM,
+            "v_pool1": ROOM,
+            "v_grouped0": ROOM,
+            "y1_codes": ROOM + 1024,
+            "y0_codes": ROOM + 2048,
+            "q_raw0": 2 * ROOM,
+            "v_pool2": 2 * ROOM,
+            "v_grouped1": 2 * ROOM,
+            "v0_codes": 2 * ROOM + 1024,
+            "q_grouped0_2": 3 * ROOM,
+            "v_pool3": 3 * ROOM,
+            "ks_listed": 4 * ROOM,
+            "q_raw1": 4 * ROOM,
+            "rs01": 4 * ROOM,
+            "rs2": 4 * ROOM + 8 * EARLY,
+            "rs3": 4 * ROOM + 12 * EARLY,
+            "rs_late": 4 * ROOM + 16 * EARLY,
+            "v3_codes": 4 * ROOM + 8 * EARLY,
+        }
 
         def sbuf(shape, dtype, name):
             if name in places:
                 return shared.tile(shape, dtype, name=name, align_bytes=64, offset=places[name])
             return keep.tile(shape, dtype, name=name, align_bytes=64)
 
-        offsets = keep.tile([P, SLOTS // 16], U16, name="offsets")
+        offsets = keep.tile([P, LIST_COLUMNS], U16, name="offsets")
         nc.sync.dma_start(offsets[:], offs)
         ks_pool = sbuf([P, NEURONS], U8, "ks_pool")
         nc.vector.memset(ks_pool[0:96, :].bitcast(I32), 0)
@@ -67,9 +90,9 @@ def tile_attend_mlp_relu2_topk_kernel(tc, qT, k_words, k_scales, vT, us, rs, off
                 out=ks_planes[32 * quad : 32 * quad + 4, :].bitcast(I32).rearrange("p (o n) -> p o n", o=PASSES),
                 in_=ks_dealt[96 + 8 * quad : 96 + 8 * (quad + 1), :].bitcast(I32),
             )
-        q_raw1 = sbuf([P, PACK, NQ], F32, "ks_listed")
+        q_raw1 = sbuf([P, PACK, NQ], F32, "q_raw1")
         nc.sync.dma_start(out=q_raw1[:], in_=q_rows[1])
-        kw_listed = sbuf([P, SLOTS], U32, "ks_pool")
+        kw_listed = sbuf([P, SLOTS], U32, "kw_listed")
         nc.vector.tensor_copy(kw_listed[:], kw_pool[:].bitcast(U32).indirect(offsets[:]))
         kw_dealt = sbuf([P, PASSES * SLOTS * 2], U8, "kw_dealt")
         nc.vector.tensor_copy(
@@ -80,8 +103,6 @@ def tile_attend_mlp_relu2_topk_kernel(tc, qT, k_words, k_scales, vT, us, rs, off
         ident = sbuf([P, P], F32, "ident")
         make_identity(nc, ident[:])
 
-        q_mx = {}
-
         def round_q(raw, copy, name):
             grouped = sbuf([P, raw.shape[2] * PACK], BF16, name)
             copy(
@@ -90,168 +111,134 @@ def tile_attend_mlp_relu2_topk_kernel(tc, qT, k_words, k_scales, vT, us, rs, off
             )
             return grouped
 
-        def quantize(grouped, width, name, codes=None):
-            if codes is None:
-                codes = sbuf([P, width], U32, f"{name}_codes")
+        def quantize(grouped, width, name):
+            codes = sbuf([P, width], U32, f"{name}_codes")
             scales = sbuf([P, width], U8, f"{name}_scales")
             nc.vector.quantize_mx(out=codes[:].bitcast(FP8X4), scales=scales[:], in_=grouped)
-            return codes, scales
+            return [(codes[:, at : at + P], scales[:, at : at + P]) for at in range(0, width, P)]
 
-        def quantize_q0(h, grouped, codes=None):
-            codes, scales = quantize(grouped[:], 2 * P, f"q0_{h}", codes)
-            for n in range(2):
-                q_mx[(0, 2 * h + n)] = (codes[:, P * n : P * (n + 1)], scales[:, P * n : P * (n + 1)])
+        engines_copy = (nc.vector.tensor_copy, nc.scalar.copy)
+        q0 = [round_q(q_raw0[:, :, P * c : P * (c + 1)], nc.vector.tensor_copy, f"q_grouped0_{c}") for c in range(2)]
+        q0.append(round_q(q_raw0[:, :, 2 * P : NQ], nc.scalar.copy, "q_grouped0_2"))
+        q0_mx = quantize(q0[0][:], P, "q0_0") + quantize(q0[1][:], P, "q0_1") + quantize(q0[2][:], 2 * P, "q0_2")
+        q1 = [round_q(q_raw1[:, :, P * c : P * (c + 1)], engines_copy[c % 2], f"q_grouped1_{c}") for c in range(Q_TILES)]
+        q1_mx = [quantize(q1[c][:], P, f"q1_{c}")[0] for c in range(Q_TILES)]
 
-        def round_q1(c, copy):
-            return round_q(q_raw1[:, :, P * c : P * (c + 1)], copy, f"q_grouped1_{c}")
-
-        def quantize_q1(c, grouped):
-            codes, scales = quantize(grouped[:], P, f"q1_{c}")
-            q_mx[(1, c)] = (codes[:], scales[:])
-
-        q0_low = round_q(q_raw0[:, :, 0 : 2 * P], nc.vector.tensor_copy, "q_grouped0_0")
-        q0_high = round_q(q_raw0[:, :, 2 * P : NQ], nc.scalar.copy, "q_grouped0_1")
-        quantize_q0(0, q0_low)
-        quantize_q0(1, q0_high)
-        q1 = [round_q1(c, (nc.vector.tensor_copy, nc.scalar.copy)[c % 2]) for c in range(Q_TILES)]
+        scores = [psum.tile([P, PACK, P], F32, name=f"bank{c}") for c in range(Q_TILES)]
         for c in range(Q_TILES):
-            quantize_q1(c, q1[c])
-
-        a_banks = [psum.tile([P, PACK, P], F32, name=f"bank{c}") for c in range(Q_TILES)]
-        for c in range(Q_TILES):
-            for o in range(PASSES):
+            for o, q_mx in enumerate((q0_mx, q1_mx)):
                 for t in range(PACK):
                     at = (o * PACK + t) * P
                     nc.tensor.matmul_mx(
-                        out=a_banks[c][:, t, :],
+                        out=scores[c][:, t, :],
                         lhsT=kw_dealt[:, 2 * at : 2 * (at + P)].bitcast(FP4X4),
                         lhsT_scale=ks_planes[:, at : at + P],
-                        rhs=q_mx[(o, c)][0].bitcast(FP8X4),
-                        rhs_scale=q_mx[(o, c)][1],
+                        rhs=q_mx[c][0].bitcast(FP8X4),
+                        rhs_scale=q_mx[c][1],
                         start=(o == 0 and t == 0),
                         stop=(o == PASSES - 1 and t == PACK - 1),
                     )
 
-        v_pool = [sbuf([P, NEURONS], F32, name) for name in ("kw_pool", "ks_pool", "v_pool2", "ks_listed")]
+        v_pool = [sbuf([P, NEURONS], F32, f"v_pool{j}") for j in range(E_BLOCKS)]
         for j in range(E_BLOCKS):
             nc.sync.dma_start(out=v_pool[j][:], in_=vT[P * j : P * (j + 1), :])
 
         rs_rows = rs[0].rearrange("(c p) e -> p c e", p=P)
-        pairs = [slice(0, 2), slice(2, 4)]
-        rs_sb = sbuf([P, Q_TILES, DV], F32, "q_grouped1_3")
-        for pair in pairs:
-            nc.sync.dma_start(out=rs_sb[:, pair, :], in_=rs_rows[:, pair, :])
+        rs01 = sbuf([P, 2, EARLY], F32, "rs01")
+        nc.sync.dma_start(out=rs01[:], in_=rs_rows[:, 0:2, 0:EARLY])
+        rs_early = [rs01[:, 0, :], rs01[:, 1, :]]
+        for c in (2, 3):
+            rows = sbuf([P, EARLY], F32, f"rs{c}")
+            nc.sync.dma_start(out=rows[:], in_=rs_rows[:, c, 0:EARLY])
+            rs_early.append(rows[:])
+        rs_late = sbuf([P, Q_TILES, P], F32, "rs_late")
+        nc.sync.dma_start(out=rs_late[:], in_=rs_rows[:, :, EARLY:DV])
 
-        def gather_v(j, vector_columns):
-            listed = sbuf([P, SLOTS], BF16, f"v_listed{j}")
-            cut = 16 * vector_columns
-            if vector_columns > 0:
-                nc.vector.tensor_copy(listed[:, 0:cut], v_pool[j][:].indirect(offsets[:, 0:vector_columns]))
-            if vector_columns < LIST_COLUMNS:
-                nc.scalar.activation(
-                    out=listed[:, cut:SLOTS],
-                    in_=v_pool[j][:].indirect(offsets[:, vector_columns:LIST_COLUMNS]),
-                    func=ACT.Copy,
-                )
+        us_along_q = us_cols[:].unsqueeze(1).to_broadcast([P, P, PACK])
+        y_grouped = [sbuf([P, 2, P, PACK], BF16, f"y_grouped{parity}") for parity in range(2)]
+        a = [bank[:].rearrange("p t q -> p q t") for bank in scores]
+
+        halves = [slice(0, P // 2), slice(P // 2, P)]
+        for c in (0, 2):
+            squared = sbuf([P, P, PACK], F32, f"squared{c}")
+            relus = [sbuf([P, P // 2, PACK], F32, f"relu{h}") for h in range(2)]
+            for relu, half in zip(relus, halves):
+                nc.scalar.activation(out=relu[:], in_=a[c][:, half, :], func=ACT.Relu)
+            for relu, half in zip(relus, halves):
+                nc.scalar.activation(out=squared[:, half, :], in_=relu[:], func=ACT.Square)
+            nc.gpsimd.tensor_tensor(out=y_grouped[0][:, c // 2, :, :], in0=squared[:], in1=us_along_q, op=ALU.mult)
+        weighed = {c: sbuf([P, P, PACK], F32, f"weighed{c}") for c in (1, 3)}
+        for c in (1, 3):
+            nc.vector.scalar_tensor_tensor(
+                out=weighed[c][:], in0=a[c], scalar=0.0, in1=us_along_q, op0=ALU.max, op1=ALU.mult
+            )
+        for c in (1, 3):
+            nc.vector.tensor_tensor(out=y_grouped[1][:, c // 2, :, :], in0=a[c], in1=weighed[c][:], op=ALU.mult)
+
+        def gather_v(j):
+            listed = sbuf([P, SLOTS], BF16, f"v_listed{j}" if j > 0 else "relu0")
+            columns = VECTOR_COLUMNS[j]
+            nc.vector.tensor_copy(listed[:, 0 : 16 * columns], v_pool[j][:].indirect(offsets[:, 0:columns]))
+            nc.scalar.activation(
+                out=listed[:, 16 * columns : SLOTS],
+                in_=v_pool[j][:].indirect(offsets[:, columns:LIST_COLUMNS]),
+                func=ACT.Copy,
+            )
             return listed
 
-        def turn_v(j, listed, grouped):
+        def turn_v(j, listed):
             turned = psum.tile([P, 2, P], F32, name=f"bank{4 + j % 2}")
             words = listed[:].bitcast(F32)
             for u in range(2):
                 nc.tensor.transpose(turned[:, u, :], words[:, u : 2 * P : 2], ident[:])
+            grouped = sbuf([P, P * PACK], BF16, f"v_grouped{j}")
             nc.scalar.copy(
-                out=grouped.bitcast(F32).rearrange("p (e u) -> p e u", u=2),
+                out=grouped[:].bitcast(F32).rearrange("p (e u) -> p e u", u=2),
                 in_=turned[:].rearrange("p u e -> p e u"),
             )
+            return grouped
 
-        def second_product(acc, c, v_mx):
-            tile_codes, tile_scales = y_mx[c]
+        def product(acc, c, v_mx):
             nc.tensor.matmul_mx(
                 out=acc,
-                lhsT=tile_codes.bitcast(FP8X4),
-                lhsT_scale=tile_scales,
-                rhs=v_mx[0][:].bitcast(FP8X4),
-                rhs_scale=v_mx[1][:],
+                lhsT=y_mx[c][0].bitcast(FP8X4),
+                lhsT_scale=y_mx[c][1],
+                rhs=v_mx[0].bitcast(FP8X4),
+                rhs_scale=v_mx[1],
                 start=True,
                 stop=True,
             )
 
-        us_along_q = us_cols[:].unsqueeze(1).to_broadcast([P, P, PACK])
-        y_grouped = sbuf([P, Q_TILES, P, PACK], BF16, "y_grouped")
-
-        def weigh_on_vector(c, name):
-            scores = a_banks[c][:].rearrange("p t q -> p q t")
-            weighed = sbuf([P, P, PACK], F32, name)
-            nc.vector.scalar_tensor_tensor(
-                out=weighed[:], in0=scores, scalar=0.0, in1=us_along_q, op0=ALU.max, op1=ALU.mult
-            )
-            nc.vector.tensor_tensor(out=y_grouped[:, c, :, :], in0=scores, in1=weighed[:], op=ALU.mult)
-
-        def weigh_on_gpsimd(c):
-            scores = a_banks[c][:].rearrange("p t q -> p q t")
-            squared = sbuf([P, P, PACK], F32, f"squared{c}")
-            halves = [slice(0, P // 2), slice(P // 2, P)]
-            relus = [sbuf([P, P // 2, PACK], F32, f"relu{h}") for h in range(2)]
-            for relu, half in zip(relus, halves):
-                nc.scalar.activation(out=relu[:], in_=scores[:, half, :], func=ACT.Relu)
-            for relu, half in zip(relus, halves):
-                nc.scalar.activation(out=squared[:, half, :], in_=relu[:], func=ACT.Square)
-            nc.gpsimd.tensor_tensor(out=y_grouped[:, c, :, :], in0=squared[:], in1=us_along_q, op=ALU.mult)
-
-        weigh_on_gpsimd(0)
-        weigh_on_vector(1, "weighed1")
-        weigh_on_gpsimd(2)
-        weigh_on_gpsimd(3)
-        listed = [gather_v(j, LIST_COLUMNS) for j in range(2)]
-        v0_grouped = sbuf([P, P * PACK], BF16, "relu1")
-        turn_v(0, listed[0], v0_grouped[:])
-        listed.append(gather_v(2, 16))
-        y_mx = []
-
-        def quantize_y(h):
-            codes, scales = quantize(y_grouped[:, pairs[h], :, :].rearrange("p c q t -> p (c q t)"), 2 * P, f"y{h}")
-            y_mx.extend([(codes[:, P * n : P * (n + 1)], scales[:, P * n : P * (n + 1)]) for n in range(2)])
-
-        quantize_y(0)
-
-        def quantize_early(j, grouped):
-            columns = slice(P * j, P * (j + 1))
-            nc.vector.quantize_mx(out=v01_codes[:, columns].bitcast(FP8X4), scales=v01_scales[:, columns], in_=grouped[:])
-
-        v01_codes = sbuf([P, HALF], U32, "v01_codes")
-        v01_scales = sbuf([P, HALF], U8, "v01_scales")
-        quantize_early(0, v0_grouped)
-        v1_grouped = sbuf([P, P * PACK], BF16, "v1_grouped")
-        turn_v(1, listed[1], v1_grouped[:])
-        v2_grouped = sbuf([P, P * PACK], BF16, "v2_grouped")
-        turn_v(2, listed[2], v2_grouped[:])
-        quantize_early(1, v1_grouped)
-        quantize_y(1)
-        early_banks = [psum.tile([P, 2, HALF], F32, name=f"bank{2 * h}") for h in range(2)]
-        for c in range(Q_TILES):
-            second_product(early_banks[c // 2][:, c % 2, :], c, (v01_codes, v01_scales))
-        listed.append(gather_v(3, 16))
-        v3_grouped = sbuf([P, P * PACK], BF16, "v3_grouped")
-        turn_v(3, listed[3], v3_grouped[:])
-
         out_rows = out[0].rearrange("(c p) e -> p c e", p=P)
 
-        def finish(bank, tiles, columns, name):
-            result = sbuf(list(bank.shape), F32, name)
-            nc.vector.tensor_tensor(out=result[:], in0=bank, in1=rs_sb[:, tiles, columns], op=ALU.add)
-            nc.sync.dma_start(out=out_rows[:, tiles, columns], in_=result[:])
+        def finish(bank, residual, rows, name):
+            result = sbuf(list(residual.shape), F32, name)
+            nc.vector.tensor_tensor(out=result[:], in0=bank, in1=residual, op=ALU.add)
+            nc.sync.dma_start(out=rows, in_=result[:])
 
-        v2 = quantize(v2_grouped[:], P, "v2", sbuf([P, P], U32, "ks_listed"))
-        banks2 = [psum.tile([P, 2, P], F32, name=name) for name in ("bank1", "bank3")]
-        for c in range(Q_TILES):
-            second_product(banks2[c // 2][:, c % 2, :], c, v2)
-        finish(early_banks[0][:], pairs[0], slice(0, HALF), "early0")
-        finish(banks2[0][:], pairs[0], slice(HALF, 3 * P), "middle0")
-        v3 = quantize(v3_grouped[:], P, "v3")
-        finish(early_banks[1][:], pairs[1], slice(0, HALF), "early1")
-        finish(banks2[1][:], pairs[1], slice(HALF, 3 * P), "middle1")
-        bank3 = psum.tile([P, Q_TILES, P], F32, name="bank6")
-        for c in range(Q_TILES):
-            second_product(bank3[:, c, :], c, v3)
-        finish(bank3[:], slice(0, Q_TILES), slice(3 * P, DV), "late")
+        def finish_tile(c):
+            finish(sums[c][:], rs_early[c], out_rows[:, c, 0:EARLY], f"result{c}")
+
+        listed = [gather_v(j) for j in range(2)]
+        odd, even = [
+            quantize(y_grouped[parity][:].rearrange("p c q t -> p (c q t)"), 2 * P, f"y{parity}") for parity in (1, 0)
+        ]
+        y_mx = [even[0], odd[0], even[1], odd[1]]
+        sums = [psum.tile([P, EARLY], F32, name=f"bank{c}") for c in range(Q_TILES)]
+        for j in range(E_BLOCKS - 1):
+            if j == 1:
+                listed.append(gather_v(2))
+            v_mx = quantize(turn_v(j, listed[j])[:], P, f"v{j}")[0]
+            for c in range(Q_TILES):
+                product(sums[c][:, P * j : P * (j + 1)], c, v_mx)
+        grouped3 = turn_v(3, gather_v(3))
+        for c in range(3):
+            finish_tile(c)
+        v_mx = quantize(grouped3[:], P, "v3")[0]
+        finish_tile(3)
+        for h in range(2):
+            pair = slice(2 * h, 2 * h + 2)
+            late = psum.tile([P, 2, P], F32, name=f"bank{6 + h}")
+            for n in range(2):
+                product(late[:, n, :], 2 * h + n, v_mx)
+            finish(late[:], rs_late[:, pair, :], out_rows[:, pair, EARLY:DV], f"result_late{h}")

@@ -20,10 +20,10 @@ SLOTS, NEURONS, D, NQ, DV = 512, 2048, 1024, 512, 512
 PASSES = D // (P * PACK)
 Q_TILES = NQ // P
 E_BLOCKS = DV // P
-EARLY = DV - P
+HALF = DV // 2
 LIST_COLUMNS = SLOTS // 16
 ROOM = 4 * NEURONS
-VECTOR_COLUMNS = (14, 14, 16, 14)
+VECTOR_COLUMNS = (14, 14, 16, 16)
 
 FLOPS = 2 * SLOTS * NQ * (D + DV)
 
@@ -51,11 +51,11 @@ def tile_attend_mlp_relu2_topk_kernel(tc, qT, k_words, k_scales, vT, us, rs, off
             "v_pool3": 3 * ROOM,
             "ks_listed": 4 * ROOM,
             "q_raw1": 4 * ROOM,
-            "rs01": 4 * ROOM,
-            "rs2": 4 * ROOM + 8 * EARLY,
-            "rs3": 4 * ROOM + 12 * EARLY,
-            "rs_late": 4 * ROOM + 16 * EARLY,
-            "v3_codes": 4 * ROOM + 8 * EARLY,
+            "v2_codes": 3 * ROOM,
+            "rs_early0": 4 * ROOM,
+            "rs_early1": 4 * ROOM + 8 * HALF,
+            "rs_late": 4 * ROOM + 16 * HALF,
+            "v3_codes": 4 * ROOM,
         }
 
         def sbuf(shape, dtype, name):
@@ -144,15 +144,12 @@ def tile_attend_mlp_relu2_topk_kernel(tc, qT, k_words, k_scales, vT, us, rs, off
             nc.sync.dma_start(out=v_pool[j][:], in_=vT[P * j : P * (j + 1), :])
 
         rs_rows = rs[0].rearrange("(c p) e -> p c e", p=P)
-        rs01 = sbuf([P, 2, EARLY], F32, "rs01")
-        nc.sync.dma_start(out=rs01[:], in_=rs_rows[:, 0:2, 0:EARLY])
-        rs_early = [rs01[:, 0, :], rs01[:, 1, :]]
-        for c in (2, 3):
-            rows = sbuf([P, EARLY], F32, f"rs{c}")
-            nc.sync.dma_start(out=rows[:], in_=rs_rows[:, c, 0:EARLY])
-            rs_early.append(rows[:])
-        rs_late = sbuf([P, Q_TILES, P], F32, "rs_late")
-        nc.sync.dma_start(out=rs_late[:], in_=rs_rows[:, :, EARLY:DV])
+        pairs = [slice(0, 2), slice(2, 4)]
+        rs_early = [sbuf([P, 2, HALF], F32, f"rs_early{h}") for h in range(2)]
+        for h in range(2):
+            nc.sync.dma_start(out=rs_early[h][:], in_=rs_rows[:, pairs[h], 0:HALF])
+        rs_late = sbuf([P, Q_TILES, HALF], F32, "rs_late")
+        nc.sync.dma_start(out=rs_late[:], in_=rs_rows[:, :, HALF:DV])
 
         us_along_q = us_cols[:].unsqueeze(1).to_broadcast([P, P, PACK])
         y_grouped = [sbuf([P, 2, P, PACK], BF16, f"y_grouped{parity}") for parity in range(2)]
@@ -216,29 +213,30 @@ def tile_attend_mlp_relu2_topk_kernel(tc, qT, k_words, k_scales, vT, us, rs, off
             nc.vector.tensor_tensor(out=result[:], in0=bank, in1=residual, op=ALU.add)
             nc.sync.dma_start(out=rows, in_=result[:])
 
-        def finish_tile(c):
-            finish(sums[c][:], rs_early[c], out_rows[:, c, 0:EARLY], f"result{c}")
-
         listed = [gather_v(j) for j in range(2)]
         odd, even = [
             quantize(y_grouped[parity][:].rearrange("p c q t -> p (c q t)"), 2 * P, f"y{parity}") for parity in (1, 0)
         ]
         y_mx = [even[0], odd[0], even[1], odd[1]]
-        sums = [psum.tile([P, EARLY], F32, name=f"bank{c}") for c in range(Q_TILES)]
-        for j in range(E_BLOCKS - 1):
+        early = [psum.tile([P, 2, HALF], F32, name=f"bank{2 * h}") for h in range(2)]
+        for j in range(2):
             if j == 1:
                 listed.append(gather_v(2))
             v_mx = quantize(turn_v(j, listed[j])[:], P, f"v{j}")[0]
             for c in range(Q_TILES):
-                product(sums[c][:, P * j : P * (j + 1)], c, v_mx)
+                product(early[c // 2][:, c % 2, P * j : P * (j + 1)], c, v_mx)
+        grouped2 = turn_v(2, listed[2])
         grouped3 = turn_v(3, gather_v(3))
-        for c in range(3):
-            finish_tile(c)
-        v_mx = quantize(grouped3[:], P, "v3")[0]
-        finish_tile(3)
+        v_mx = quantize(grouped2[:], P, "v2")[0]
+        middle = psum.tile([P, Q_TILES, P], F32, name="bank1")
+        for c in range(Q_TILES):
+            product(middle[:, c, :], c, v_mx)
         for h in range(2):
-            pair = slice(2 * h, 2 * h + 2)
+            finish(early[h][:], rs_early[h][:], out_rows[:, pairs[h], 0:HALF], f"result_early{h}")
+        v_mx = quantize(grouped3[:], P, "v3")[0]
+        finish(middle[:], rs_late[:, :, 0:P], out_rows[:, :, HALF : HALF + P], "result_middle")
+        for h in range(2):
             late = psum.tile([P, 2, P], F32, name=f"bank{6 + h}")
             for n in range(2):
                 product(late[:, n, :], 2 * h + n, v_mx)
-            finish(late[:], rs_late[:, pair, :], out_rows[:, pair, EARLY:DV], f"result_late{h}")
+            finish(late[:], rs_late[:, pairs[h], P:HALF], out_rows[:, pairs[h], HALF + P : DV], f"result_late{h}")

@@ -23,7 +23,7 @@ E_BLOCKS = DV // P
 HALF = DV // 2
 LIST_COLUMNS = SLOTS // 16
 ROOM = 4 * NEURONS
-VECTOR_COLUMNS = (14, 14, 16, 16)
+VECTOR_COLUMNS = (14, 14, 16, 12)
 
 FLOPS = 2 * SLOTS * NQ * (D + DV)
 
@@ -51,11 +51,11 @@ def tile_attend_mlp_relu2_topk_kernel(tc, qT, k_words, k_scales, vT, us, rs, off
             "v_pool3": 3 * ROOM,
             "ks_listed": 4 * ROOM,
             "q_raw1": 4 * ROOM,
-            "v2_codes": 3 * ROOM,
             "rs_early0": 4 * ROOM,
             "rs_early1": 4 * ROOM + 8 * HALF,
-            "rs_late": 4 * ROOM + 16 * HALF,
-            "v3_codes": 4 * ROOM,
+            "rs_late0": 4 * ROOM + 16 * HALF,
+            "rs_late1": 4 * ROOM + 24 * HALF,
+            "v3_codes": 4 * ROOM + 8 * HALF,
         }
 
         def sbuf(shape, dtype, name):
@@ -148,8 +148,9 @@ def tile_attend_mlp_relu2_topk_kernel(tc, qT, k_words, k_scales, vT, us, rs, off
         rs_early = [sbuf([P, 2, HALF], F32, f"rs_early{h}") for h in range(2)]
         for h in range(2):
             nc.sync.dma_start(out=rs_early[h][:], in_=rs_rows[:, pairs[h], 0:HALF])
-        rs_late = sbuf([P, Q_TILES, HALF], F32, "rs_late")
-        nc.sync.dma_start(out=rs_late[:], in_=rs_rows[:, :, HALF:DV])
+        rs_late = [sbuf([P, 2, HALF], F32, f"rs_late{h}") for h in range(2)]
+        for h in range(2):
+            nc.sync.dma_start(out=rs_late[h][:], in_=rs_rows[:, pairs[h], HALF:DV])
 
         us_along_q = us_cols[:].unsqueeze(1).to_broadcast([P, P, PACK])
         y_grouped = [sbuf([P, 2, P, PACK], BF16, f"y_grouped{parity}") for parity in range(2)]
@@ -225,18 +226,29 @@ def tile_attend_mlp_relu2_topk_kernel(tc, qT, k_words, k_scales, vT, us, rs, off
             v_mx = quantize(turn_v(j, listed[j])[:], P, f"v{j}")[0]
             for c in range(Q_TILES):
                 product(early[c // 2][:, c % 2, P * j : P * (j + 1)], c, v_mx)
-        grouped2 = turn_v(2, listed[2])
+        v_mx = quantize(turn_v(2, listed[2])[:], P, "v2")[0]
+        middle = [psum.tile([P, 2, P], F32, name="bank1")]
+        for n in range(2):
+            product(middle[0][:, n, :], n, v_mx)
         grouped3 = turn_v(3, gather_v(3))
-        v_mx = quantize(grouped2[:], P, "v2")[0]
-        middle = psum.tile([P, Q_TILES, P], F32, name="bank1")
-        for c in range(Q_TILES):
-            product(middle[:, c, :], c, v_mx)
-        for h in range(2):
+
+        def finish_early(h):
             finish(early[h][:], rs_early[h][:], out_rows[:, pairs[h], 0:HALF], f"result_early{h}")
+
+        finish_early(0)
+        middle.append(psum.tile([P, 2, P], F32, name="bank0"))
+        for n in range(2):
+            product(middle[1][:, n, :], 2 + n, v_mx)
+
+        def finish_middle(h):
+            finish(middle[h][:], rs_late[h][:, :, 0:P], out_rows[:, pairs[h], HALF : HALF + P], f"result_middle{h}")
+
+        finish_early(1)
+        finish_middle(0)
         v_mx = quantize(grouped3[:], P, "v3")[0]
-        finish(middle[:], rs_late[:, :, 0:P], out_rows[:, :, HALF : HALF + P], "result_middle")
+        finish_middle(1)
         for h in range(2):
             late = psum.tile([P, 2, P], F32, name=f"bank{6 + h}")
             for n in range(2):
                 product(late[:, n, :], 2 * h + n, v_mx)
-            finish(late[:], rs_late[:, pairs[h], P:HALF], out_rows[:, pairs[h], HALF + P : DV], f"result_late{h}")
+            finish(late[:], rs_late[h][:, :, P:HALF], out_rows[:, pairs[h], HALF + P : DV], f"result_late{h}")

@@ -85,7 +85,7 @@ def tile_attend_mlp_relu2_topk_kernel(tc, qT, k_words, k_scales, vT, us, rs, off
             ks_dealt[:].rearrange("p (t m) -> p t m", t=PACK),
             ks_listed[:].rearrange("p (m t) -> p t m", t=PACK),
         )
-        for quad in range(4):
+        for quad in (0, 2, 1, 3):
             nc.sync.dma_start(
                 out=ks_planes[32 * quad : 32 * quad + 4, :].bitcast(I32).rearrange("p (o n) -> p o n", o=PASSES),
                 in_=ks_dealt[96 + 8 * quad : 96 + 8 * (quad + 1), :].bitcast(I32),

from contextlib import ExitStack

import concourse.mybir as mybir
from concourse.masks import make_identity

F32 = mybir.dt.float32
BF16 = mybir.dt.bfloat16
I32 = mybir.dt.int32
U32 = mybir.dt.uint32
U16 = mybir.dt.uint16
U8 = mybir.dt.uint8
FP8X4 = mybir.dt.float8_e4m3fn_x4
FP4X4 = mybir.dt.float4_e2m1fn_x4
ACT = mybir.ActivationFunctionType
ALU = mybir.AluOpType

P = 128
PACK = 4
SLOTS, NEURONS, D, NQ, DV = 512, 2048, 1024, 512, 512
PASSES = D // (P * PACK)
Q_TILES = NQ // P
E_BLOCKS = DV // P
HALF = DV // 2
LIST_COLUMNS = SLOTS // 16
ROOM = 4 * NEURONS
VECTOR_COLUMNS = (14, 14, 16, 12)

FLOPS = 2 * SLOTS * NQ * (D + DV)


def tile_attend_mlp_relu2_topk_kernel(tc, qT, k_words, k_scales, vT, us, rs, offs, out):
    nc = tc.nc
    with ExitStack() as ctx:
        keep = ctx.enter_context(tc.tile_pool(name="keep", bufs=1))
        psum = ctx.enter_context(tc.psum_pool(name="psum", bufs=1))
        shared = ctx.enter_context(tc.tile_pool(name="shared", bufs=1))
        places = {
            "kw_pool": 0,
            "v_pool0": 0,
            "ks_pool": ROOM,
            "kw_listed": ROOM,
            "v_pool1": ROOM,
            "v_grouped0": ROOM,
            "y1_codes": ROOM + 1024,
            "y0_codes": ROOM + 2048,
            "q_raw0": 2 * ROOM,
            "v_pool2": 2 * ROOM,
            "v_grouped1": 2 * ROOM,
            "v0_codes": 2 * ROOM + 1024,
            "q_grouped0_2": 3 * ROOM,
            "v_pool3": 3 * ROOM,
            "ks_listed": 4 * ROOM,
            "q_raw1": 4 * ROOM,
            "rs_early0": 4 * ROOM,
            "rs_early1": 4 * ROOM + 8 * HALF,
            "rs_late0": 4 * ROOM + 16 * HALF,
            "rs_late1": 4 * ROOM + 24 * HALF,
            "v3_codes": 4 * ROOM + 8 * HALF,
        }

        def sbuf(shape, dtype, name):
            if name in places:
                return shared.tile(shape, dtype, name=name, align_bytes=64, offset=places[name])
            return keep.tile(shape, dtype, name=name, align_bytes=64)

        offsets = keep.tile([P, LIST_COLUMNS], U16, name="offsets")
        nc.sync.dma_start(offsets[:], offs)
        ks_pool = sbuf([P, NEURONS], U8, "ks_pool")
        nc.vector.memset(ks_pool[0:96, :].bitcast(I32), 0)
        nc.sync.dma_start(out=ks_pool[96:P, :].bitcast(I32), in_=k_scales.bitcast(I32).rearrange("o f n -> f o n"))
        kw_pool = sbuf([P, NEURONS], I32, "kw_pool")
        nc.sync.dma_start(out=kw_pool[:], in_=k_words[0].rearrange("p n b -> p (n b)").bitcast(I32))
        ks_planes = sbuf([P, PASSES * SLOTS], U8, "ks_planes")
        nc.vector.memset(ks_planes[:].bitcast(I32), 0)
        q_rows = qT[0].rearrange("(o p t) q -> o p t q", o=PASSES, t=PACK)
        q_raw0 = sbuf([P, PACK, NQ], F32, "q_raw0")
        nc.sync.dma_start(out=q_raw0[:], in_=q_rows[0])
        us_cols = sbuf([P, PACK], F32, "us_cols")
        nc.sync.dma_start(out=us_cols[:], in_=us[0].rearrange("(p t) one -> p (t one)", t=PACK))

        ks_listed = sbuf([P, SLOTS], U8, "ks_listed")
        nc.vector.tensor_copy(ks_listed[:], ks_pool[:].indirect(offsets[:]))
        ks_dealt = sbuf([P, SLOTS], U8, "ks_dealt")
        nc.vector.tensor_copy(
            ks_dealt[:].rearrange("p (t m) -> p t m", t=PACK),
            ks_listed[:].rearrange("p (m t) -> p t m", t=PACK),
        )
        for quad in (0, 2, 1, 3):
            nc.sync.dma_start(
                out=ks_planes[32 * quad : 32 * quad + 4, :].bitcast(I32).rearrange("p (o n) -> p o n", o=PASSES),
                in_=ks_dealt[96 + 8 * quad : 96 + 8 * (quad + 1), :].bitcast(I32),
            )
        q_raw1 = sbuf([P, PACK, NQ], F32, "q_raw1")
        nc.sync.dma_start(out=q_raw1[:], in_=q_rows[1])
        kw_listed = sbuf([P, SLOTS], U32, "kw_listed")
        nc.vector.tensor_copy(kw_listed[:], kw_pool[:].bitcast(U32).indirect(offsets[:]))
        kw_dealt = sbuf([P, PASSES * SLOTS * 2], U8, "kw_dealt")
        nc.vector.tensor_copy(
            kw_dealt[:].bitcast(U16).rearrange("p (o t m) -> p o m t", o=PASSES, t=PACK),
            kw_listed[:].bitcast(U16).rearrange("p (m t o) -> p o m t", o=PASSES, t=PACK),
        )

        ident = sbuf([P, P], F32, "ident")
        make_identity(nc, ident[:])

        def round_q(raw, copy, name):
            grouped = sbuf([P, raw.shape[2] * PACK], BF16, name)
            copy(
                out=grouped[:].rearrange("p (c i t) -> p c t i", i=4, t=PACK),
                in_=raw.rearrange("p t (c i) -> p c t i", i=4),
            )
            return grouped

        def quantize(grouped, width, name):
            codes = sbuf([P, width], U32, f"{name}_codes")
            scales = sbuf([P, width], U8, f"{name}_scales")
            nc.vector.quantize_mx(out=codes[:].bitcast(FP8X4), scales=scales[:], in_=grouped)
            return [(codes[:, at : at + P], scales[:, at : at + P]) for at in range(0, width, P)]

        engines_copy = (nc.vector.tensor_copy, nc.scalar.copy)
        q0 = [round_q(q_raw0[:, :, P * c : P * (c + 1)], nc.vector.tensor_copy, f"q_grouped0_{c}") for c in range(2)]
        q0.append(round_q(q_raw0[:, :, 2 * P : NQ], nc.scalar.copy, "q_grouped0_2"))
        q0_mx = quantize(q0[0][:], P, "q0_0") + quantize(q0[1][:], P, "q0_1") + quantize(q0[2][:], 2 * P, "q0_2")
        q1 = [round_q(q_raw1[:, :, P * c : P * (c + 1)], engines_copy[c % 2], f"q_grouped1_{c}") for c in range(Q_TILES)]
        q1_mx = [quantize(q1[c][:], P, f"q1_{c}")[0] for c in range(Q_TILES)]

        scores = [psum.tile([P, PACK, P], F32, name=f"bank{c}") for c in range(Q_TILES)]
        for c in range(Q_TILES):
            for o, q_mx in enumerate((q0_mx, q1_mx)):
                for t in range(PACK):
                    at = (o * PACK + t) * P
                    nc.tensor.matmul_mx(
                        out=scores[c][:, t, :],
                        lhsT=kw_dealt[:, 2 * at : 2 * (at + P)].bitcast(FP4X4),
                        lhsT_scale=ks_planes[:, at : at + P],
                        rhs=q_mx[c][0].bitcast(FP8X4),
                        rhs_scale=q_mx[c][1],
                        start=(o == 0 and t == 0),
                        stop=(o == PASSES - 1 and t == PACK - 1),
                    )

        v_pool = [sbuf([P, NEURONS], F32, f"v_pool{j}") for j in range(E_BLOCKS)]
        for j in range(E_BLOCKS):
            nc.sync.dma_start(out=v_pool[j][:], in_=vT[P * j : P * (j + 1), :])

        rs_rows = rs[0].rearrange("(c p) e -> p c e", p=P)
        pairs = [slice(0, 2), slice(2, 4)]
        rs_early = [sbuf([P, 2, HALF], F32, f"rs_early{h}") for h in range(2)]
        for h in range(2):
            nc.sync.dma_start(out=rs_early[h][:], in_=rs_rows[:, pairs[h], 0:HALF])
        rs_late = [sbuf([P, 2, HALF], F32, f"rs_late{h}") for h in range(2)]
        for h in range(2):
            nc.sync.dma_start(out=rs_late[h][:], in_=rs_rows[:, pairs[h], HALF:DV])

        us_along_q = us_cols[:].unsqueeze(1).to_broadcast([P, P, PACK])
        y_grouped = [sbuf([P, 2, P, PACK], BF16, f"y_grouped{parity}") for parity in range(2)]
        a = [bank[:].rearrange("p t q -> p q t") for bank in scores]

        halves = [slice(0, P // 2), slice(P // 2, P)]
        for c in (0, 2):
            squared = sbuf([P, P, PACK], F32, f"squared{c}")
            relus = [sbuf([P, P // 2, PACK], F32, f"relu{h}") for h in range(2)]
            for relu, half in zip(relus, halves):
                nc.scalar.activation(out=relu[:], in_=a[c][:, half, :], func=ACT.Relu)
            for relu, half in zip(relus, halves):
                nc.scalar.activation(out=squared[:, half, :], in_=relu[:], func=ACT.Square)
            nc.gpsimd.tensor_tensor(out=y_grouped[0][:, c // 2, :, :], in0=squared[:], in1=us_along_q, op=ALU.mult)
        weighed = {c: sbuf([P, P, PACK], F32, f"weighed{c}") for c in (1, 3)}
        for c in (1, 3):
            nc.vector.scalar_tensor_tensor(
                out=weighed[c][:], in0=a[c], scalar=0.0, in1=us_along_q, op0=ALU.max, op1=ALU.mult
            )
        for c in (1, 3):
            nc.vector.tensor_tensor(out=y_grouped[1][:, c // 2, :, :], in0=a[c], in1=weighed[c][:], op=ALU.mult)

        def gather_v(j):
            listed = sbuf([P, SLOTS], BF16, f"v_listed{j}" if j > 0 else "relu0")
            columns = VECTOR_COLUMNS[j]
            nc.vector.tensor_copy(listed[:, 0 : 16 * columns], v_pool[j][:].indirect(offsets[:, 0:columns]))
            nc.scalar.activation(
                out=listed[:, 16 * columns : SLOTS],
                in_=v_pool[j][:].indirect(offsets[:, columns:LIST_COLUMNS]),
                func=ACT.Copy,
            )
            return listed

        def turn_v(j, listed):
            turned = psum.tile([P, 2, P], F32, name=f"bank{4 + j % 2}")
            words = listed[:].bitcast(F32)
            for u in range(2):
                nc.tensor.transpose(turned[:, u, :], words[:, u : 2 * P : 2], ident[:])
            grouped = sbuf([P, P * PACK], BF16, f"v_grouped{j}")
            nc.scalar.copy(
                out=grouped[:].bitcast(F32).rearrange("p (e u) -> p e u", u=2),
                in_=turned[:].rearrange("p u e -> p e u"),
            )
            return grouped

        def product(acc, c, v_mx):
            nc.tensor.matmul_mx(
                out=acc,
                lhsT=y_mx[c][0].bitcast(FP8X4),
                lhsT_scale=y_mx[c][1],
                rhs=v_mx[0].bitcast(FP8X4),
                rhs_scale=v_mx[1],
                start=True,
                stop=True,
            )

        out_rows = out[0].rearrange("(c p) e -> p c e", p=P)

        def finish(bank, residual, rows, name):
            result = sbuf(list(residual.shape), F32, name)
            nc.vector.tensor_tensor(out=result[:], in0=bank, in1=residual, op=ALU.add)
            nc.sync.dma_start(out=rows, in_=result[:])

        listed = [gather_v(j) for j in range(2)]
        odd, even = [
            quantize(y_grouped[parity][:].rearrange("p c q t -> p (c q t)"), 2 * P, f"y{parity}") for parity in (1, 0)
        ]
        y_mx = [even[0], odd[0], even[1], odd[1]]
        early = [psum.tile([P, 2, HALF], F32, name=f"bank{2 * h}") for h in range(2)]
        for j in range(2):
            if j == 1:
                listed.append(gather_v(2))
            v_mx = quantize(turn_v(j, listed[j])[:], P, f"v{j}")[0]
            for c in range(Q_TILES):
                product(early[c // 2][:, c % 2, P * j : P * (j + 1)], c, v_mx)
        v_mx = quantize(turn_v(2, listed[2])[:], P, "v2")[0]
        middle = [psum.tile([P, 2, P], F32, name="bank1")]
        for n in range(2):
            product(middle[0][:, n, :], n, v_mx)
        grouped3 = turn_v(3, gather_v(3))

        def finish_early(h):
            finish(early[h][:], rs_early[h][:], out_rows[:, pairs[h], 0:HALF], f"result_early{h}")

        finish_early(0)
        middle.append(psum.tile([P, 2, P], F32, name="bank0"))
        for n in range(2):
            product(middle[1][:, n, :], 2 + n, v_mx)

        def finish_middle(h):
            finish(middle[h][:], rs_late[h][:, :, 0:P], out_rows[:, pairs[h], HALF : HALF + P], f"result_middle{h}")

        finish_early(1)
        finish_middle(0)
        v_mx = quantize(grouped3[:], P, "v3")[0]
        finish_middle(1)
        for h in range(2):
            late = psum.tile([P, 2, P], F32, name=f"bank{6 + h}")
            for n in range(2):
                product(late[:, n, :], 2 * h + n, v_mx)
            finish(late[:], rs_late[h][:, :, P:HALF], out_rows[:, pairs[h], HALF + P : DV], f"result_late{h}")
